import numpy as np, ml_dtypes
CORES = [16,18,20,22]
N = 4
import mx_ref
BF = ml_dtypes.bfloat16
def cols(t, e):
    v = np.concatenate([t.reshape(128, -1, 4), np.zeros((128, 1, 4), BF)], axis=1)
    return np.ascontiguousarray(v[:, e]).reshape(128, -1)
def cut(t, i, w=512):
    return t[:, w * i:w * i + w]
def pick(q, e):
    c = np.concatenate([q[0].reshape(128, -1, 4), np.zeros((128, 1, 4), np.uint8)], axis=1); s = np.concatenate([q[1], np.ones((16, 1), np.uint8)], axis=1)
    return (np.ascontiguousarray(c[:, e].reshape(128, -1)), np.ascontiguousarray(s[:, e]))
def join(*qs):
    return (np.concatenate([q[0] for q in qs], axis=1), np.concatenate([q[1] for q in qs], axis=1))
def put(q, e, v):
    c, s = q[0].reshape(128, -1, 4).copy(), q[1].copy(); c[:, e] = v[0].reshape(128, -1, 4); s[:, e] = v[1]
    return (c.reshape(128, -1), s)
def pk(c, s):
    return (np.ascontiguousarray(c), mx_ref.live(s))
def emit(q):
    return q[0], q[1]
def decode(q):
    o = []
    for b in range(4):
        e = np.zeros((128, 128, 4), np.float32); e[np.arange(128), np.arange(128), b] = 1
        o.append(mx_ref.matmul(mx_ref.quantize(e.reshape(128, 512).astype(BF)), q))
    return np.stack(o, axis=2).reshape(128, -1)
def f(rng, *shape):
    return mx_ref.flush((rng.standard_normal(shape, dtype=np.float32) * np.exp2(rng.integers(-2, 3, shape[:-1] + (1,)))).astype(BF))
def wide(rng, *shape, cols=0):
    v = rng.standard_normal(shape, dtype=np.float32) * np.exp2(rng.integers(-12, 13, shape)).astype(np.float32)
    if cols: v *= np.repeat(np.exp2(rng.integers(-cols, cols + 1, shape[:-2] + (1, shape[-1] // 4))) * (rng.random(shape[:-2] + (1, shape[-1] // 4)) > 0.0625), 4, axis=-1).astype(np.float32)
    return mx_ref.flush(v.astype(BF))
C, R, O = 384, 2, 2
def sized(v, k=1):
    v = np.asarray(v).astype(np.float32) * np.asarray(k, np.float32)
    v[np.abs(v) < np.float32(2.0 ** -8)] = 0
    return v.astype(BF)
def alike(t):
    return np.repeat(t[None], N, axis=0)
def setup_inputs(rng):
    k = np.exp2(rng.integers(1, 6, (N, 1, C)))
    return {"x": sized(f(rng, N, 128, 4 * C), np.repeat(k, 4, axis=2)), "b": alike(sized(f(rng, 128, 512), 8)), "w": f(rng, N, 128, 512 * O)}
def setup_inputs_ties(rng):
    d = setup_inputs(rng)
    x = np.stack([cols(d["x"][r], rng.permutation(C) % 24 - 1) for r in range(N)])
    z, e = int(rng.integers(0, N)), np.full(C, -1)
    e[int(rng.integers(0, C))] = 0
    x[z] = cols(d["x"][z], e)
    return {"x": x, "b": alike(cols(d["b"][0], rng.permutation(128) % 12 - 1)), "w": d["w"]}
def setup_inputs_near(rng):
    p = rng.choice([-1.0, 1.0], (128, 64, 4))
    k = np.sort(rng.permutation(128).reshape(64, 2), axis=1)
    b = np.zeros((128, 128, 4))
    b[:, k[:, 0]] = p
    b[:, k[:, 1]] = p
    b[:8] = 0
    b[120:] = 0
    b[127, k[:, 1], 3] = 1
    x = np.zeros((N, 128, C, 4))
    for r in range(N):
        v = 0.5 * rng.choice([-1.0, 1.0], (128, C, 4))
        j = np.sort(rng.permutation(C)[:128].reshape(64, 2), axis=1)
        v[:, j[:, 0]] = p
        v[:, j[:, 1]] = p
        v[120:] = 0
        v[127, j[:, 1], 3] = 2.0 ** -14
        x[r] = v * 2.0 ** int(rng.integers(8, 12))
    x[0, :8] = 2.0 ** 27
    x[1:N - 1, :8] = rng.choice([-1.0, 1.0], (N - 2, 8, C, 4)) * rng.integers(1, 16, (N - 2, 8, C, 4))
    x[N - 1, :8] = -2.0 ** 27
    return {"x": sized(x.reshape(N, 128, 4 * C)), "b": alike(sized(b.reshape(128, 512))), "w": f(rng, N, 128, 512 * O)}
def setup_inputs_low(rng):
    sign = np.ones(N)
    sign[rng.permutation(N)[:N // 4]] = -1
    def far(*shape):
        return (1 + rng.random(shape)) * np.exp2(rng.integers(28, 30, shape))
    return {"x": sized(far(N, 128, 4 * C), sign[:, None, None]), "b": alike(sized(far(128, 512), -1)), "w": f(rng, N, 128, 512 * O)}
def setup_inputs_lone(rng):
    q = rng.choice([-1.0, 1.0], (128, C, 4)) * rng.integers(4, 8, (128, C, 4))
    h = int(rng.integers(0, N))
    x = np.stack([q[:, rng.permutation(C)] * (16.0 if r == h else 1.0) for r in range(N)])
    b = sized(f(rng, 128, 4), 8).astype(np.float32)[:, None, :] * np.exp2(rng.integers(0, 6, (1, 128, 1)))
    return {"x": sized(x.reshape(N, 128, 4 * C)), "b": alike(sized(b.reshape(128, 512))), "w": f(rng, N, 128, 512 * O)}
def setup_inputs_spread(rng):
    return {"x": sized(wide(rng, N, 128, 4 * C, cols=6), 64), "b": alike(sized(wide(rng, 128, 512, cols=4), 64)), "w": f(rng, N, 128, 512 * O)}
def check_inputs(d):
    bad = []
    for k, low in (("x", 2.0 ** -8), ("b", 2.0 ** -30), ("w", 2.0 ** -30)):
        v = np.abs(d[k].astype(np.float32))
        if not (np.isfinite(v).all() and ((v == 0) | (v >= low) & (v <= 2.0 ** 30)).all()): bad.append("a value of " + k)
    v = d["b"].astype(np.float32)
    if (v != v[:1]).any(): bad.append("b differs between ranks")
    return bad
def match(g):
    g = g + np.float32(0)
    j, k = np.argmax(g, axis=1), np.argmax(g, axis=0)
    both = k[j] == np.arange(128)
    e = j.copy()
    e[~both] = np.setdiff1d(np.arange(C), j[both])[:np.sum(~both)]
    return e, both
def reference(x, b, w):
    T = [mx_ref.quantize(np.ascontiguousarray(x[r])) for r in range(N)]
    B = mx_ref.quantize(np.ascontiguousarray(b[0]))
    pa = np.zeros((N, R, 128), np.float32)
    for t in range(R):
        m = [match(mx_ref.matmul(B, T[r])) for r in range(N)]
        v = [decode(pick(T[r], m[r][0])) for r in range(N)]
        s = v[0]
        for r in range(1, N): s = s + v[r]
        B = mx_ref.quantize((s * np.float32(0.25)).astype(BF))
        d = decode(B)
        for r in range(N):
            e, both = m[r]
            pa[r, t] = e
            new = mx_ref.quantize(((v[r] + d) * np.float32(0.5)).astype(BF))
            T[r] = put(T[r], e[both], pick(new, np.flatnonzero(both)))
    y = np.zeros((N, 128, O * (C + 128)), np.float32)
    oc, osc = np.zeros((N, 128, 4 * C), np.uint8), np.zeros((N, 16, C), np.uint8)
    for r in range(N):
        for o in range(O):
            i = o * (C + 128)
            y[r, :, i:i + C + 128] = mx_ref.matmul(mx_ref.quantize(np.ascontiguousarray(cut(w[r], o))), join(T[r], B))
        oc[r], osc[r] = emit(T[r])
    return {"y": y, "oc": oc, "osc": osc, "pa": pa}

@@ -1,0 +1,399 @@
+from concourse.bass import DstId, RemoteDMATransfer
+from concourse.mybir import dt, AluOpType as A, ActivationFunctionType as F
+
+C = 384
+N = 4
+LAST = N - 1
+BIG = 1.5 * 2.0 ** 28
+
+SCRATCH = {"ps": ("psum", [128, 4096], "float32")}
+for _n, _w in (("xt", 1536), ("bt", 512), ("wt", 1024), ("dd", 128), ("rr", 128), ("fm", 128), ("kk", 128),
+               ("nd", 128), ("ni", 128), ("neg", 128), ("one", 516), ("uu", 516), ("jt", 1536), ("tt", 1536),
+               ("ww", 1536), ("tmp", 128), ("at", 512), ("vt", 512), ("dz", 384), ("junk", 384), ("sg", 128)):
+    SCRATCH[_n] = ("sbuf", [128, _w], "bfloat16")
+for _n, _w in (("pc", 384), ("pr", 384), ("la", 384), ("sel", 128), ("cs", 128), ("tl", 768), ("val", 128),
+               ("selt", 384), ("cl", 32), ("pas", 256), ("ysb", 1024)):
+    SCRATCH[_n] = ("sbuf", [128, _w], "float32")
+for _n, _w in (("wa", 512), ("wb", 512), ("tc", 384), ("b0", 128), ("b1q", 128), ("b1l", 128), ("b2q", 128),
+               ("b2l", 128), ("p1", 128), ("p2", 128), ("l1", 512), ("l2", 512), ("jq", 384), ("eq", 512),
+               ("zq", 128), ("t2q", 128), ("t3q", 128), ("w2q", 128), ("w3q", 128), ("w4q", 128), ("wq", 256)):
+    SCRATCH[_n] = ("sbuf", [128, _w], "float8_e4m3fn_x4")
+    SCRATCH[_n + "s"] = ("sbuf", [128, _w], "uint8")
+for _n, _w in (("off1", 8), ("off2", 8), ("tof1", 24), ("tof2", 24)):
+    SCRATCH[_n] = ("sbuf", [128, _w], "uint16")
+
+SEMAPHORES = ["cv", "cs", "cp", "cg", "db", "dx0", "dx2", "dw", "out", "sent",
+              "ar0", "ar1", "ar2", "ar3", "arb"]
+COUNTER = {"v": "cv", "s": "cs", "p": "cp", "g": "cg"}
+
+
+def make_plan():
+    return {"ops": [], "wr": {}, "rd": {}, "bank": {}, "n": {}}
+
+
+def note(pl, q, fn, reads=(), writes=(), banks=(), sem=None, inc=0):
+    deps = []
+    for k in reads:
+        if k in pl["wr"]:
+            deps.append(pl["wr"][k])
+    for k in writes:
+        if k in pl["wr"]:
+            deps.append(pl["wr"][k])
+        deps.extend(pl["rd"].get(k, []))
+    for b in banks:
+        if b in pl["bank"] and pl["bank"][b][1] != q:
+            deps.append(pl["bank"][b])
+    if sem is None:
+        pl["n"][q] = pl["n"].get(q, 0) + 1
+        tok = ("c", q, pl["n"][q])
+    else:
+        pl["n"][sem] = pl["n"].get(sem, 0) + inc
+        tok = ("d", sem, pl["n"][sem])
+    pl["ops"].append((q, fn, deps, tok))
+    for k in reads:
+        pl["rd"].setdefault(k, []).append(tok)
+    for k in writes:
+        pl["wr"][k] = tok
+        pl["rd"][k] = []
+    for b in banks:
+        pl["bank"][b] = tok
+    return tok
+
+
+def emit(pl, queues, T, ends):
+    known, clock, waits, needed = {}, {}, [], set()
+    for q, fn, deps, tok in pl["ops"]:
+        kn = known.setdefault(q, {})
+        best = {}
+        for d in deps:
+            best[d[:2]] = max(best.get(d[:2], 0), d[2])
+        order = sorted(best.items(), key=lambda e: -len(clock.get(e[0] + (e[1],), {})))
+        mine = []
+        for key, val in order:
+            if kn.get(key, 0) >= val:
+                continue
+            mine.append(key + (val,))
+            kn[key] = val
+            for k2, v2 in clock.get(key + (val,), {}).items():
+                kn[k2] = max(kn.get(k2, 0), v2)
+        waits.append(mine)
+        needed.update(w for w in mine if w[0] == "c")
+        clock[tok] = dict(kn)
+    count, seen = {}, {}
+    for q, fn, deps, tok in pl["ops"]:
+        if tok in needed:
+            seen[q] = seen.get(q, 0) + 1
+            count[tok] = seen[q]
+    for (q, fn, deps, tok), mine in zip(pl["ops"], waits):
+        for w in mine:
+            if w[0] == "c":
+                queues[q].wait_ge(T.sem[COUNTER[w[1]]], count[w])
+            else:
+                queues[q].wait_ge(T.sem[w[1]], w[2])
+        ins = fn()
+        if tok in needed:
+            ins.then_inc(T.sem[COUNTER[q]], 1)
+    for q, sem in ends:
+        if pl["n"].get(sem, 0):
+            queues[q].wait_ge(T.sem[sem], pl["n"][sem])
+
+
+def rank_program(g, core, T, topo):
+    rank = T.rank_of(core)
+    if rank is None:
+        return
+    cores = list(T.cores)
+    V, S, P, Y = g.vector, g.scalar, g.tensor, g.sync
+    queues = {"v": V, "s": S, "p": P, "g": g, "y": Y}
+    pl = make_plan()
+    u8, u32 = dt.uint8, dt.uint32
+
+    def bank(b, n=128):
+        return T.ps[:, 512 * b:512 * b + n]
+
+    def col(i):
+        return T.cl[:, i:i + 1]
+    KB, JB, HH, UU, T1, P2, TQ, Q32, NPM, CORR, V4, T4 = 0, 3, 4, 5, 6, 7, 8, 9, 10, 11, 12, 13
+
+    def slot(buf, piece, t, pieces=1):
+        return T[buf][:, 512 * piece + t:512 * (piece + pieces):4]
+
+    def ts(out, in0, s1, s2, op0, op1, r, w, banks=()):
+        if op1 is None:
+            note(pl, "v", lambda: V.tensor_scalar(out, in0, s1, None, op0), r, w, banks)
+        else:
+            note(pl, "v", lambda: V.tensor_scalar(out, in0, s1, s2, op0, op1), r, w, banks)
+
+    def act(out, in_, func, scale, bias, r, w, banks=(), accum=None):
+        if accum is None:
+            note(pl, "s", lambda: S.activation(out, in_, func, bias=bias, scale=scale), r, w, banks)
+        else:
+            note(pl, "s", lambda: S.activation(out, in_, func, bias=bias, scale=scale, accum_out=accum), r, w, banks)
+
+    def fill(ap, c, w):
+        note(pl, "v", lambda: V.memset(ap, c), (), w)
+
+    def scan(out, d0, d1, init, op0, op1, r, w, banks=()):
+        note(pl, "v", lambda: V.tensor_tensor_scan(out, d0, d1, init, op0, op1), r, w, banks)
+
+    def quant(name, a, n, src, r, w):
+        note(pl, "v", lambda: V.quantize_mx(T[name][:, a:a + n], T[name + "s"][:, a:a + n], src), r, w)
+
+    def mm(b, st, sa, mv, ma, n, start, stop, r):
+        note(pl, "p", lambda: P.matmul_mx(bank(b, n), T[st][:, sa:sa + 128], T[st + "s"][:, sa:sa + 128],
+                                          T[mv][:, ma:ma + n], T[mv + "s"][:, ma:ma + n], start, stop), r, (), (b,))
+
+    def pick(dst, a, n, win, wn, off, r, w):
+        o = T[off][:, a // 16:(a + n) // 16]
+        note(pl, "v", lambda: V.tensor_copy(T[dst][:, a:a + n].bitcast(u32),
+                                            T[win][:, 0:wn].bitcast(u32).indirect(o)), r, [w + "c"])
+        note(pl, "s", lambda: S.activation(T[dst + "s"][:, a:a + n], T[win + "s"][:, 0:wn].indirect(o), F.Copy),
+             r, [w + "s"])
+
+    def dma(q, out, in_, r, w, sem):
+        note(pl, q, lambda: queues[q].dma_start(out, in_).then_inc(T.sem[sem], 16), r, w, sem=sem, inc=16)
+
+    def lanes(src, dsts):
+        m = topo.mask(cores[src], cores[dsts[0]])
+        for d in dsts[1:]:
+            m &= topo.mask(cores[src], cores[d])
+        return m, bin(m).count("1")
+
+    def write(src, dst, dsts, sem, r):
+        m, n = lanes(rank, dsts)
+        ids = [DstId(rid=topo.addr(cores[d])[0], pnc=topo.addr(cores[d])[1]) for d in dsts]
+        tr = RemoteDMATransfer(dst_ids=ids, dma_engine_mask=m, remote_sem=T.sem[sem], src=src,
+                               dsts=[dst for d in dsts])
+        note(pl, "g", lambda: g.remote_dma_fused([tr], local_sem=T.sem.sent), r, (), sem="sent", inc=n)
+
+    def arrives(key, sem, n):
+        pl["wr"][key] = ("d", sem, n)
+
+    dma("y", T.bt[:], T.b[:], (), ["bt"], "db")
+    dma("s", T.xt[:, 0:1024], T.x[:, 0:1024], (), ["xt0", "xt1"], "dx0")
+    dma("y", T.xt[:, 1024:1536], T.x[:, 1024:1536], (), ["xt2"], "dx2")
+    dma("y", T.wt[:], T.w[:], ["xt1", "xt2"], ["wt"], "dw")
+
+    def iota(out, pat, base, cm, w):
+        note(pl, "g", lambda: g.iota(out, pat, base, cm, allow_small_or_imprecise_dtypes=True), (), w)
+
+    def sel_g(out, in_, pat, op, c, base, cm, r, w):
+        note(pl, "g", lambda: g.affine_select(out, in_, pat, op, c, base, cm), r, w)
+
+    fill(T.one[:], 1.0, ["one"])
+    fill(T.neg[:], -1.0, ["neg"])
+    iota(T.dd[:], [[1, 128]], 0, -1, ["dd"])
+    iota(T.rr[:], [[1, 128]], 0, 0, ["rr"])
+    sel_g(T.tmp[:], T.neg[:], [[1, 128]], A.is_ge, 0.0, 0, -1, ["neg"], ["tmp"])
+    sel_g(slot("ww", 0, 1), T.tmp[:], [[1, 128]], A.not_equal, -256.0, 0, -1, ["tmp"], ["w2s1"])
+    iota(col(P2), [[1, 1]], -15, 2, ["p2c"])
+    iota(T.fm[:], [[0, 8], [2, 16]], -15, 0, ["fm"])
+    sel_g(T.ni[:], T.neg[:], [[1, 128]], A.is_equal, -4096.0, 0, -1, ["neg"], ["ni"])
+    iota(col(V4), [[1, 1]], C, 1, ["v4"])
+    sel_g(T.uu[:], T.one[:], [[1, 516]], A.is_equal, 0.0, -3, -4, ["one"], ["uu"])
+    iota(T.tl[:], [[0, 2], [1, C]], 0, 0, ["tl0", "tl1"])
+
+    fill(slot("jt", 1, 0, 2), 0.0, ["jz0"])
+    fill(slot("jt", 0, 2, 2), 0.0, ["jz1"])
+    fill(slot("jt", 0, 1), 0.0, ["jz2"])
+    fill(slot("jt", 2, 1), 0.0, ["jz3"])
+    fill(T.dz[:, 0:1], 0.0, ["dz0"])
+    for i in range(3):
+        ts(slot("jt", i, i), T.dd[:], 0.0, None, A.is_equal, None, ["dd"], ["ji%d" % i])
+        ts(slot("jt", i, 3), T.dd[:], 0.0, float(i), A.is_ge, A.add, ["dd"], ["jn%d" % i])
+    quant("jq", 0, C, T.jt[:], ["jz0", "jz1", "jz2", "jz3", "ji0", "ji1", "ji2", "jn0", "jn1", "jn2"], ["jq"])
+
+    act(slot("ww", 0, 0, 3), T.one[:, 0:C], F.Copy, 0.25, 0.0, ["one"], ["ws0"])
+    act(slot("ww", 0, 3, 3), T.one[:, 0:C], F.Copy, 0.0, 0.0, ["one"], ["ws3"])
+    act(slot("ww", 0, 2), T.one[:, 0:128], F.Copy, 0.0, 0.0, ["one"], ["w2s2"])
+    quant("w2q", 0, 128, T.ww[:, 0:512], ["ws0", "ws3", "w2s1", "w2s2"], ["w2q"])
+    act(slot("tt", 0, 3, 3), T.one[:, 0:C], F.Copy, 0.5, 0.0, ["one"], ["ts3"])
+    act(slot("tt", 1, 2), T.one[:, 0:128], F.Copy, 0.0, 0.0, ["one"], ["t2s2"])
+    act(T.kk[:], T.rr[:], F.Copy, 1.0 / 2048, 0.0, ["rr"], ["kk"])
+    act(T.nd[:], T.dd[:], F.Copy, -0.25, 0.0, ["dd"], ["nd"])
+    act(col(TQ), col(P2), F.Identity, 1.0, BIG, ["p2c"], ["tq"])
+    act(col(Q32), col(TQ), F.Identity, 1.0, -BIG, ["tq"], ["q32"])
+    act(col(NPM), col(P2), F.Identity, -1.0, col(Q32), ["q32", "p2c"], ["npm"])
+    act(T.sg[:], T.fm[:], F.Sign, 1.0, col(NPM), ["fm", "npm"], ["sg"])
+    act(col(CORR), col(NPM), F.Identity, 512.0, 7680.0, ["npm"], ["corr"])
+    act(T.cs[:], T.sg[:], F.Identity, 33792.0, -32768.0, ["sg"], ["cs"])
+
+    def digits(piece, value, t, key, name):
+        act(col(t), col(value), F.Identity, 1.0, BIG, [key], [name + "t"])
+        act(slot("ww", piece, 1), T.one[:, 0:128], F.Identity, -BIG, col(t), ["one", name + "t"], [name + "1"])
+        act(slot("ww", piece, 2), slot("ww", piece, 1), F.Identity, -1.0, col(value), [name + "1", key], [name + "2"])
+
+    def quant_x(i):
+        quant("wa", 128 * i, 128, T.xt[:, 512 * i:512 * i + 512], ["xt%d" % i], ["t0p%d" % i])
+
+    def quant_w():
+        quant("wq", 0, 256, T.wt[:], ["wt"], ["wq"])
+
+    def best_place(i):
+        a = 128 * i
+        scan(T.pc[:, a:a + 128], bank(i), T.one[:, 0:128], -1e29, A.max, A.mult, ["one"], ["pc%d" % i], (i,))
+        act(T.junk[:, a:a + 128], T.pc[:, a:a + 128], F.Sign, -1.0, T.pc[:, a + 127:a + 128], ["pc%d" % i],
+            ["kb%d" % i, "junk%d" % i], accum=col(KB + i))
+
+    pat, pkeys = "b0", ["b0"]
+    tkeys = [["t0p0"], ["t0p1"], ["t0p2"]]
+    for t in range(2):
+        tab, pk, off, tof = ("wa", "p1", "off1", "tof1") if t == 0 else ("wb", "p2", "off2", "tof2")
+        land = "l1" if t == 0 else "l2"
+        tall = sorted(set(tkeys[0] + tkeys[1] + tkeys[2]))
+        summers = [r for r in range(N) if r != LAST] if t == 0 else [LAST]
+
+        if t == 0:
+            quant("b0", 0, 128, T.bt[:], ["bt"], ["b0"])
+            quant_x(0)
+            quant_x(1)
+            for i in range(2):
+                mm(i, tab, 128 * i, pat, 0, 128, True, True, tkeys[i] + pkeys)
+            mm(3, pat, 0, tab, 0, 256, True, True, tkeys[0] + tkeys[1] + pkeys)
+            best_place(0)
+            best_place(1)
+            quant_x(2)
+            mm(2, tab, 256, pat, 0, 128, True, True, tkeys[2] + pkeys)
+            mm(5, pat, 0, tab, 256, 128, True, True, tkeys[2] + pkeys)
+            scan(T.pr[:, 0:256], bank(3, 256), T.one[:, 0:256], -1e29, A.max, A.mult, ["one"], ["pra"], (3,))
+            best_place(2)
+            scan(T.pr[:, 256:C], bank(5), T.one[:, 0:128], T.pr[:, 255:256], A.max, A.mult, ["one", "pra"], ["pr"], (5,))
+        else:
+            for i in range(3):
+                mm(i, tab, 128 * i, pat, 0, 128, True, True, tkeys[i] + pkeys)
+            mm(3, pat, 0, tab, 0, C, True, True, tall + pkeys)
+            for i in range(3):
+                best_place(i)
+            scan(T.pr[:], bank(3, C), T.one[:, 0:C], -1e29, A.max, A.mult, ["one"], ["pr", "pra"], (3,))
+        act(T.dz[:, 1:C], T.pr[:, 0:C - 1], F.Sign, -1.0, T.pr[:, C - 1:C], ["pr", "pra"], ["dz", "jb"],
+            accum=col(JB))
+        for i in range(3):
+            ts(slot("tt", 0, i), T.rr[:], col(KB + i), -0.25, A.is_equal, A.mult, ["rr", "kb%d" % i], ["z%d" % i])
+        quant("zq", 0, 128, T.tt[:, 0:512], ["z0", "z1", "z2", "ts3"], ["zq"])
+        mm(4, "zq", 0, "jq", 0, C, True, True, ["zq", "jq"])
+        ts(col(HH), col(JB), 0.5 - 1.0 / 2048, 0.25, A.mult, A.add, ["jb"], ["hh"])
+        ts(col(UU), col(JB), 0.5, 0.5, A.mult, A.add, ["jb"], ["uc"])
+        digits(1, JB, T1, "jb", "w3")
+        scan(T.la[:], T.dz[:], bank(4, C), 1e4, A.add, A.min, ["dz", "dz0"], ["la"], (4,))
+        f = T.la[:, C - 1:C]
+        ts(slot("tt", 1, 0), T.kk[:], col(HH), f, A.add, A.is_ge, ["kk", "hh", "la"], ["t2s0"])
+        act(slot("tt", 1, 1), T.neg[:], F.Identity, f, col(UU), ["neg", "uc", "la"], ["t2s1"])
+        quant("t2q", 0, 128, T.tt[:, 512:1024], ["t2s0", "t2s1", "t2s2", "ts3"], ["t2q"])
+        mm(5, "t2q", 0, "w2q", 0, 128, True, True, ["t2q", "w2q"])
+        for s in (1, 2):
+            act(slot("tt", 2, s), T.ni[:], F.Relu, f, col(UU), ["ni", "uc", "la"], ["t3s%d" % s])
+        quant("w3q", 0, 128, T.ww[:, 512:1024], ["ws0", "ws3", "w31", "w32"], ["w3q"])
+        note(pl, "v", lambda: V.tensor_tensor(slot("tt", 2, 0), bank(5), T.nd[:], A.is_gt), ["nd"], ["t3s0"], (5,))
+        quant("t3q", 0, 128, T.tt[:, 1024:1536], ["t3s0", "t3s1", "t3s2", "ts3"], ["t3q"])
+        mm(6, "w3q", 0, "t3q", 0, 128, True, True, ["w3q", "t3q"])
+        scan(T.sel[:], T.cs[:], bank(6), 0.0, A.add, A.max, ["cs"], ["sel"], (6,))
+        ts(T[off][:], T.sel[:, 15:128:16], col(CORR), 4.0, A.subtract, A.mult, ["sel", "corr"], [off])
+        pick(pk, 0, 128, tab, C, off, tall + [off], pk)
+        own = [pk + "c", pk + "s"]
+
+        dsts = [r for r in summers if r != rank]
+        if dsts:
+            a = 128 * rank
+            write(T[pk][:].bitcast(u8), T[land][:, a:a + 128].bitcast(u8), dsts, "ar%d" % rank, [pk + "c"])
+            write(T[pk + "s"][:], T[land + "s"][:, a:a + 128], dsts, "ar%d" % rank, [pk + "s"])
+
+        act(T.pas[0:1, 128 * t:128 * t + 128], T.ps[0:1, 3072:3200], F.Copy, 4.0, 0.0, (), ["pas%d" % t], (6,))
+        if t == 0:
+            digits(2, V4, T4, "v4", "w4")
+            for b in range(4):
+                quant("eq", 128 * b, 128, T.uu[:, 3 - b:515 - b], ["uu"], ["e%d" % b])
+            quant("w4q", 0, 128, T.ww[:, 1024:1536], ["ws0", "ws3", "w41", "w42"], ["w4q"])
+        mm(7, "w4q", 0, "t3q", 0, 128, True, True, ["w4q", "t3q"])
+        act(T.val[:], bank(7), F.Copy, 4.0, 0.0, (), ["val"], (7,))
+
+        def table_list(t=t, off=off, tof=tof):
+            win = T.tl[:, C * t:C * t + C]
+            note(pl, "v", lambda: V.tensor_copy(win.indirect(T[off][:]), T.val[:]), ["val", off], ["tl%d" % t])
+            for i in range(3):
+                scan(T.selt[:, 128 * i:128 * i + 128], T.cs[:], T.tl[:, C * t + 128 * i:C * t + 128 * i + 128], 0.0,
+                     A.add, A.max, ["cs", "tl%d" % t], ["selt%d" % i])
+            ts(T[tof][:], T.selt[:, 15:C:16], col(CORR), None, A.subtract, None,
+               ["selt0", "selt1", "selt2", "corr"], [tof])
+
+        def held(pk=pk, own=own):
+            for b in range(4):
+                mm(4 + b, "eq", 128 * b, pk, 0, 128, True, False, ["e%d" % b] + own)
+
+        def evacuate(first, tile, c, name):
+            for b in range(4):
+                if b % 2 == 0:
+                    ts(slot(tile, 0, b), bank(first + b), c, None, A.mult, None, (), [name + str(b)], (first + b,))
+                else:
+                    act(slot(tile, 0, b), bank(first + b), F.Copy, c, 0.0, (), [name + str(b)], (first + b,))
+            return [name + str(b) for b in range(4)]
+
+        late = t == 1 and rank == LAST
+        if not late:
+            table_list()
+            held()
+            if (t == 0) == (rank == LAST):
+                quant_w()
+
+        if rank in summers:
+            order = [1, 0, 2, 3] if rank == 1 else [0, 1, 2, 3]
+            for n, r in enumerate(order):
+                if r == rank:
+                    mv, a, keys = pk, 0, own
+                else:
+                    arrives("land%d" % r, "ar%d" % r, 2 * lanes(r, [d for d in summers if d != r])[1])
+                    mv, a, keys = land, 128 * r, ["land%d" % r]
+                for b in range(4):
+                    mm(b, "eq", 128 * b, mv, a, 128, n == 0, n == N - 1, ["e%d" % b] + keys)
+            pat = "b1q" if t == 0 else "b2q"
+            quant(pat, 0, 128, T.at[:], evacuate(0, "at", 0.25, "at"), [pat])
+            pkeys = [pat]
+        others = [r for r in range(N) if r not in summers]
+        far = "b1l" if t == 0 else "b2l"
+        giver = min(summers, key=lambda r: (topo.die(cores[r]) != topo.die(cores[others[0]]), -r))
+        if rank == giver:
+            write(T[pat][:].bitcast(u8), T[far][:].bitcast(u8), others, "arb", pkeys)
+            write(T[pat + "s"][:], T[far + "s"][:], others, "arb", pkeys)
+        if rank in others:
+            pat, pkeys = far, [far]
+            arrives(far, "arb", 2 * lanes(giver, others)[1])
+        if t == 1:
+            arrives("sent", "sent", pl["n"]["sent"])
+            dma("y", T.pa[:], T.pas[0:1, :], ["pas0", "pas1", "sent"], (), "out")
+        if late:
+            held()
+            table_list()
+
+        for b in range(4):
+            mm(4 + b, "eq", 128 * b, pat, 0, 128, False, True, ["e%d" % b] + pkeys)
+        if t == 1:
+            for o in range(2):
+                mm(o, "wq", 128 * o, pat, 0, 128, True, True, ["wq"] + pkeys)
+        quant(tab, C, 128, T.vt[:], evacuate(4, "vt", 0.5, "vt"), ["v%d" % t])
+        if t == 0:
+            pick("wb", 0, 256, "wa", 512, tof, tall + ["v0", tof], "t1a")
+            pick("wb", 256, 128, "wa", 512, tof, tall + ["v0", tof], "t1b")
+            tkeys = [["t1ac", "t1as"], ["t1ac", "t1as"], ["t1bc", "t1bs"]]
+
+    for o in range(2):
+        a = 512 * o + C
+        act(T.ysb[:, a:a + 128], bank(o), F.Copy, 1.0, 0.0, (), ["yb%d" % o], (o,))
+        dma("y", T.y[:, a:a + 128], T.ysb[:, a:a + 128], ["yb%d" % o], (), "out")
+    H = C // 2
+    for h in range(2):
+        pick("tc", H * h, H, "wb", 512, "tof2", tall + ["v1", "tof2"], "t2%d" % h)
+    for h in range(2):
+        for o in range(2):
+            mm(2 + 2 * h + o, "wq", 128 * o, "tc", H * h, H, True, True, ["wq", "t2%dc" % h, "t2%ds" % h])
+    dma("y", T.oc[:], T.tc[:].bitcast(u8), ["t20c", "t21c"], (), "out")
+    for k in range(2):
+        dma("y", T.osc[4 * k:4 * k + 4, :], T.tcs[32 * k:32 * k + 4, :], ["t20s", "t21s"], (), "out")
+    for h in range(2):
+        b = 2 + 2 * h
+        note(pl, "v", lambda b=b, h=h: V.tensor_copy(T.ysb[:, H * h:H * h + H], bank(b, H)), (), ["y0%d" % h], (b,))
+        act(T.ysb[:, 512 + H * h:512 + H * h + H], bank(b + 1, H), F.Copy, 1.0, 0.0, (), ["y1%d" % h], (b + 1,))
+    dma("y", T.y[:, 0:C], T.ysb[:, 0:C], ["y00", "y01"], (), "out")
+    dma("s", T.y[:, 512:512 + C], T.ysb[:, 512:512 + C], ["y10", "y11", "sent"], (), "out")
+    for k in range(2, 4):
+        dma("s", T.osc[4 * k:4 * k + 4, :], T.tcs[32 * k:32 * k + 4, :], ["t20s", "t21s"], (), "out")
+
+    emit(pl, queues, T, [("g", "sent"), ("y", "out")])

@@ -5,24 +5,25 @@ C = 384
 N = 4
 LAST = N - 1
 BIG = 1.5 * 2.0 ** 28
+OPT = {"w1": 1, "load": 1, "tail": 0}
 
 SCRATCH = {"ps": ("psum", [128, 4096], "float32")}
-for _n, _w in (("xt", 1536), ("bt", 512), ("wt", 1024), ("dd", 128), ("rr", 128), ("fm", 128), ("kk", 128),
-               ("nd", 128), ("ni", 128), ("neg", 128), ("one", 516), ("uu", 516), ("jt", 1536), ("tt", 1536),
-               ("ww", 1536), ("tmp", 128), ("at", 512), ("vt", 512), ("dz", 384), ("junk", 384), ("sg", 128)):
+for _n, _w in (("xt", 1536), ("bt", 512), ("wt", 1024), ("rr", 128), ("fm", 128), ("dd", 128),
+               ("one", 516), ("uu", 516), ("jt", 1536), ("th", 516),
+               ("xd", 256), ("ww", 2816), ("at", 512), ("vt", 512), ("dz", 384), ("sg", 128)):
     SCRATCH[_n] = ("sbuf", [128, _w], "bfloat16")
 for _n, _w in (("pc", 384), ("pr", 384), ("la", 384), ("sel", 128), ("cs", 128), ("tl", 768), ("val", 128),
                ("selt", 384), ("cl", 32), ("pas", 256), ("ysb", 1024)):
     SCRATCH[_n] = ("sbuf", [128, _w], "float32")
 for _n, _w in (("wa", 512), ("wb", 512), ("tc", 384), ("b0", 128), ("b1q", 128), ("b1l", 128), ("b2q", 128),
                ("b2l", 128), ("p1", 128), ("p2", 128), ("l1", 512), ("l2", 512), ("jq", 384), ("eq", 512),
-               ("zq", 128), ("t2q", 128), ("t3q", 128), ("w2q", 128), ("w3q", 128), ("w4q", 128), ("wq", 256)):
+               ("zq", 256), ("t2q", 128), ("t3q", 128), ("w2q", 128), ("w3q", 128), ("w4q", 128), ("wq", 256)):
     SCRATCH[_n] = ("sbuf", [128, _w], "float8_e4m3fn_x4")
     SCRATCH[_n + "s"] = ("sbuf", [128, _w], "uint8")
 for _n, _w in (("off1", 8), ("off2", 8), ("tof1", 24), ("tof2", 24)):
     SCRATCH[_n] = ("sbuf", [128, _w], "uint16")
 
-SEMAPHORES = ["cv", "cs", "cp", "cg", "db", "dx0", "dx2", "dw", "out", "sent",
+SEMAPHORES = ["cv", "cs", "cp", "cg", "db", "dx0", "dx1", "dx2", "dw", "out", "sent",
               "ar0", "ar1", "ar2", "ar3", "arb"]
 COUNTER = {"v": "cv", "s": "cs", "p": "cp", "g": "cg"}
 
@@ -113,10 +114,15 @@ def rank_program(g, core, T, topo):
 
     def col(i):
         return T.cl[:, i:i + 1]
-    KB, JB, HH, UU, T1, P2, TQ, Q32, NPM, CORR, V4, T4 = 0, 3, 4, 5, 6, 7, 8, 9, 10, 11, 12, 13
+    JB, HH, T1, P2, Q32, NPM, CORR, V4, T4 = range(9)
 
     def slot(buf, piece, t, pieces=1):
         return T[buf][:, 512 * piece + t:512 * (piece + pieces):4]
+
+    T2, W2, W3, W4, T3, XA = 0, 1, 2, 3, 4, 2560
+
+    def tile(piece):
+        return T.ww[:, 512 * piece:512 * piece + 512]
 
     def ts(out, in0, s1, s2, op0, op1, r, w, banks=()):
         if op1 is None:
@@ -153,25 +159,47 @@ def rank_program(g, core, T, topo):
     def dma(q, out, in_, r, w, sem):
         note(pl, q, lambda: queues[q].dma_start(out, in_).then_inc(T.sem[sem], 16), r, w, sem=sem, inc=16)
 
-    def lanes(src, dsts):
-        m = topo.mask(cores[src], cores[dsts[0]])
-        for d in dsts[1:]:
-            m &= topo.mask(cores[src], cores[d])
-        return m, bin(m).count("1")
+    def lanes(src, dsts, part=None):
+        es = [e for e in topo.engines(cores[src], cores[dsts[0]])
+              if all(e in topo.engines(cores[src], cores[d]) for d in dsts)]
+        if part is not None:
+            es = es[part::2]
+        return sum(1 << e for e in es), len(es)
 
-    def write(src, dst, dsts, sem, r):
-        m, n = lanes(rank, dsts)
+    def write(src, dst, dsts, sem, r, part=None):
+        m, n = lanes(rank, dsts, part)
         ids = [DstId(rid=topo.addr(cores[d])[0], pnc=topo.addr(cores[d])[1]) for d in dsts]
         tr = RemoteDMATransfer(dst_ids=ids, dma_engine_mask=m, remote_sem=T.sem[sem], src=src,
                                dsts=[dst for d in dsts])
         note(pl, "g", lambda: g.remote_dma_fused([tr], local_sem=T.sem.sent), r, (), sem="sent", inc=n)
 
-    def arrives(key, sem, n):
+    def calls(src, dsts, first):
+        if first and OPT["w1"] == 1:
+            return [(0, dsts, 0), (1, dsts, 1)]
+        if first and OPT["w1"] == 2:
+            return [(0, dsts[:2], 0), (1, dsts, 1)] + ([(0, dsts[2:], 1)] if dsts[2:] else [])
+        return [(0, dsts, None), (1, dsts, None)]
+
+    def send(name, land, a, dsts, sem, keys, first):
+        for kind, ds, part in calls(rank, dsts, first):
+            if kind == 0:
+                write(T[name][:].bitcast(u8), T[land][:, a:a + 128].bitcast(u8), ds, sem, keys[:1], part)
+            else:
+                write(T[name + "s"][:], T[land + "s"][:, a:a + 128], ds, sem, keys[-1:], part)
+
+    def arrives(key, sem, src, dsts, first):
+        n = sum(lanes(src, ds, part)[1] for kind, ds, part in calls(src, dsts, first) if rank in ds)
         pl["wr"][key] = ("d", sem, n)
 
-    dma("y", T.bt[:], T.b[:], (), ["bt"], "db")
-    dma("s", T.xt[:, 0:1024], T.x[:, 0:1024], (), ["xt0", "xt1"], "dx0")
-    dma("y", T.xt[:, 1024:1536], T.x[:, 1024:1536], (), ["xt2"], "dx2")
+    if OPT["load"] == 0:
+        dma("y", T.bt[:], T.b[:], (), ["bt"], "db")
+        dma("s", T.xt[:, 0:1024], T.x[:, 0:1024], (), ["xt0", "xt1"], "dx0")
+        dma("y", T.xt[:, 1024:1536], T.x[:, 1024:1536], (), ["xt2"], "dx2")
+    else:
+        dma("y", T.bt[:], T.b[:], (), ["bt"], "db")
+        dma("s", T.xt[:, 0:512], T.x[:, 0:512], (), ["xt0"], "dx0")
+        dma("y", T.xt[:, 512:1024], T.x[:, 512:1024], (), ["xt1"], "dx1")
+        dma("s", T.xt[:, 1024:1536], T.x[:, 1024:1536], (), ["xt2"], "dx2")
     dma("y", T.wt[:], T.w[:], ["xt1", "xt2"], ["wt"], "dw")
 
     def iota(out, pat, base, cm, w):
@@ -180,48 +208,59 @@ def rank_program(g, core, T, topo):
     def sel_g(out, in_, pat, op, c, base, cm, r, w):
         note(pl, "g", lambda: g.affine_select(out, in_, pat, op, c, base, cm), r, w)
 
+    def const(out, n, c, w):
+        act(out, T.one[:, 0:n], F.Copy, c, 0.0, ["one"], w)
+
     fill(T.one[:], 1.0, ["one"])
-    fill(T.neg[:], -1.0, ["neg"])
     iota(T.dd[:], [[1, 128]], 0, -1, ["dd"])
-    iota(T.rr[:], [[1, 128]], 0, 0, ["rr"])
-    sel_g(T.tmp[:], T.neg[:], [[1, 128]], A.is_ge, 0.0, 0, -1, ["neg"], ["tmp"])
-    sel_g(slot("ww", 0, 1), T.tmp[:], [[1, 128]], A.not_equal, -256.0, 0, -1, ["tmp"], ["w2s1"])
-    iota(col(P2), [[1, 1]], -15, 2, ["p2c"])
-    iota(T.fm[:], [[0, 8], [2, 16]], -15, 0, ["fm"])
-    sel_g(T.ni[:], T.neg[:], [[1, 128]], A.is_equal, -4096.0, 0, -1, ["neg"], ["ni"])
     iota(col(V4), [[1, 1]], C, 1, ["v4"])
-    sel_g(T.uu[:], T.one[:], [[1, 516]], A.is_equal, 0.0, -3, -4, ["one"], ["uu"])
-    iota(T.tl[:], [[0, 2], [1, C]], 0, 0, ["tl0", "tl1"])
+    iota(col(P2), [[1, 1]], -15, 2, ["p2c"])
+    iota(T.rr[:], [[1, 128]], 0, 0, ["rr"])
 
     fill(slot("jt", 1, 0, 2), 0.0, ["jz0"])
     fill(slot("jt", 0, 2, 2), 0.0, ["jz1"])
-    fill(slot("jt", 0, 1), 0.0, ["jz2"])
-    fill(slot("jt", 2, 1), 0.0, ["jz3"])
-    fill(T.dz[:, 0:1], 0.0, ["dz0"])
+    const(slot("jt", 0, 1), 128, 0.0, ["jz2"])
+    const(slot("jt", 2, 1), 128, 0.0, ["jz3"])
+    const(T.th[:, 3:516:4], 129, 0.25, ["th3"])
     for i in range(3):
-        ts(slot("jt", i, i), T.dd[:], 0.0, None, A.is_equal, None, ["dd"], ["ji%d" % i])
+        ts(slot("jt", i, i), T.dd[:], 0.0, -0.125, A.is_equal, A.mult, ["dd"], ["ji%d" % i])
         ts(slot("jt", i, 3), T.dd[:], 0.0, float(i), A.is_ge, A.add, ["dd"], ["jn%d" % i])
+    sel_g(slot("ww", W2, 2), slot("jt", 0, 3), [[1, 128]], A.not_equal, 256.0, 0, -1, ["jn0"], ["w2s2"])
+    iota(T.xd[:], [[1, 128], [0, 2]], 0, -1, ["xd"])
+    iota(T.fm[:], [[0, 8], [2, 16]], -15, 0, ["fm"])
+    sel_g(T.uu[:], T.one[:], [[1, 516]], A.is_equal, 0.0, -3, -4, ["one"], ["uu"])
+    fill(T.th[:, 0:3], 1.0, ["th1"])
     quant("jq", 0, C, T.jt[:], ["jz0", "jz1", "jz2", "jz3", "ji0", "ji1", "ji2", "jn0", "jn1", "jn2"], ["jq"])
+    const(T.dz[:, 0:1], 1, 0.0, ["dz0"])
+    const(slot("ww", W2, 0), 128, -1.0, ["w2s0"])
+    const(T.ww[:, 1:1024:2], 512, 0.0, ["z13"])
+    const(T.ww[:, XA + 1:XA + 256:2], 128, 0.0, ["xaz"])
+    const(slot("ww", W3, 0, 2), 256, 1.0, ["ws0"])
+    const(slot("ww", W3, 2, 3), C, 0.0, ["z2"])
+    iota(T.tl[:, 0:C], [[1, C]], 0, 0, ["tl0"])
 
-    act(slot("ww", 0, 0, 3), T.one[:, 0:C], F.Copy, 0.25, 0.0, ["one"], ["ws0"])
-    act(slot("ww", 0, 3, 3), T.one[:, 0:C], F.Copy, 0.0, 0.0, ["one"], ["ws3"])
-    act(slot("ww", 0, 2), T.one[:, 0:128], F.Copy, 0.0, 0.0, ["one"], ["w2s2"])
-    quant("w2q", 0, 128, T.ww[:, 0:512], ["ws0", "ws3", "w2s1", "w2s2"], ["w2q"])
-    act(slot("tt", 0, 3, 3), T.one[:, 0:C], F.Copy, 0.5, 0.0, ["one"], ["ts3"])
-    act(slot("tt", 1, 2), T.one[:, 0:128], F.Copy, 0.0, 0.0, ["one"], ["t2s2"])
-    act(T.kk[:], T.rr[:], F.Copy, 1.0 / 2048, 0.0, ["rr"], ["kk"])
-    act(T.nd[:], T.dd[:], F.Copy, -0.25, 0.0, ["dd"], ["nd"])
-    act(col(TQ), col(P2), F.Identity, 1.0, BIG, ["p2c"], ["tq"])
-    act(col(Q32), col(TQ), F.Identity, 1.0, -BIG, ["tq"], ["q32"])
-    act(col(NPM), col(P2), F.Identity, -1.0, col(Q32), ["q32", "p2c"], ["npm"])
-    act(T.sg[:], T.fm[:], F.Sign, 1.0, col(NPM), ["fm", "npm"], ["sg"])
-    act(col(CORR), col(NPM), F.Identity, 512.0, 7680.0, ["npm"], ["corr"])
-    act(T.cs[:], T.sg[:], F.Identity, 33792.0, -32768.0, ["sg"], ["cs"])
+    def later_constants():
+        quant("w2q", 0, 128, tile(W2), ["w2s0", "z13", "w2s2"], ["w2q"])
+        ts(col(Q32), col(P2), BIG, -BIG, A.add, A.add, ["p2c"], ["q32"])
+        ts(col(NPM), col(P2), -1.0, col(Q32), A.mult, A.add, ["q32", "p2c"], ["npm"])
+
+    def latch_constants():
+        act(T.sg[:], T.fm[:], F.Sign, 1.0, col(NPM), ["fm", "npm"], ["sg"])
+        act(col(CORR), col(NPM), F.Identity, 512.0, 7680.0, ["npm"], ["corr"])
+        act(T.cs[:], T.sg[:], F.Identity, 33792.0, -32768.0, ["sg"], ["cs"])
+
+    def rounded(value, t, key, name):
+        act(col(t), col(value), F.Identity, 1.0, BIG, [key], [name + "t"])
 
     def digits(piece, value, t, key, name):
-        act(col(t), col(value), F.Identity, 1.0, BIG, [key], [name + "t"])
         act(slot("ww", piece, 1), T.one[:, 0:128], F.Identity, -BIG, col(t), ["one", name + "t"], [name + "1"])
-        act(slot("ww", piece, 2), slot("ww", piece, 1), F.Identity, -1.0, col(value), [name + "1", key], [name + "2"])
+        act(slot("ww", piece, 3), slot("ww", piece, 1), F.Identity, -1.0, col(value), [name + "1", key], [name + "2"])
+
+    rounded(V4, T4, "v4", "w4")
+    digits(W4, V4, T4, "v4", "w4")
+
+    def quant_e(b):
+        quant("eq", 128 * b, 128, T.uu[:, 3 - b:515 - b], ["uu"], ["e%d" % b])
 
     def quant_x(i):
         quant("wa", 128 * i, 128, T.xt[:, 512 * i:512 * i + 512], ["xt%d" % i], ["t0p%d" % i])
@@ -232,8 +271,8 @@ def rank_program(g, core, T, topo):
     def best_place(i):
         a = 128 * i
         scan(T.pc[:, a:a + 128], bank(i), T.one[:, 0:128], -1e29, A.max, A.mult, ["one"], ["pc%d" % i], (i,))
-        act(T.junk[:, a:a + 128], T.pc[:, a:a + 128], F.Sign, -1.0, T.pc[:, a + 127:a + 128], ["pc%d" % i],
-            ["kb%d" % i, "junk%d" % i], accum=col(KB + i))
+        act(T.th[:, 4 + i:516:4], T.pc[:, a:a + 128], F.Sign, -1.0, T.pc[:, a + 127:a + 128], ["pc%d" % i],
+            ["th%dv" % i])
 
     pat, pkeys = "b0", ["b0"]
     tkeys = [["t0p0"], ["t0p1"], ["t0p2"]]
@@ -243,93 +282,102 @@ def rank_program(g, core, T, topo):
         tall = sorted(set(tkeys[0] + tkeys[1] + tkeys[2]))
         summers = [r for r in range(N) if r != LAST] if t == 0 else [LAST]
 
+        def places(i):
+            mm(i, tab, 128 * i, pat, 0, 128, True, True, tkeys[i] + pkeys)
+
         if t == 0:
             quant("b0", 0, 128, T.bt[:], ["bt"], ["b0"])
             quant_x(0)
+            places(0)
             quant_x(1)
-            for i in range(2):
-                mm(i, tab, 128 * i, pat, 0, 128, True, True, tkeys[i] + pkeys)
-            mm(3, pat, 0, tab, 0, 256, True, True, tkeys[0] + tkeys[1] + pkeys)
+            places(1)
             best_place(0)
-            best_place(1)
             quant_x(2)
-            mm(2, tab, 256, pat, 0, 128, True, True, tkeys[2] + pkeys)
-            mm(5, pat, 0, tab, 256, 128, True, True, tkeys[2] + pkeys)
-            scan(T.pr[:, 0:256], bank(3, 256), T.one[:, 0:256], -1e29, A.max, A.mult, ["one"], ["pra"], (3,))
-            best_place(2)
-            scan(T.pr[:, 256:C], bank(5), T.one[:, 0:128], T.pr[:, 255:256], A.max, A.mult, ["one", "pra"], ["pr"], (5,))
+            places(2)
         else:
             for i in range(3):
-                mm(i, tab, 128 * i, pat, 0, 128, True, True, tkeys[i] + pkeys)
-            mm(3, pat, 0, tab, 0, C, True, True, tall + pkeys)
-            for i in range(3):
-                best_place(i)
-            scan(T.pr[:], bank(3, C), T.one[:, 0:C], -1e29, A.max, A.mult, ["one"], ["pr", "pra"], (3,))
-        act(T.dz[:, 1:C], T.pr[:, 0:C - 1], F.Sign, -1.0, T.pr[:, C - 1:C], ["pr", "pra"], ["dz", "jb"],
-            accum=col(JB))
-        for i in range(3):
-            ts(slot("tt", 0, i), T.rr[:], col(KB + i), -0.25, A.is_equal, A.mult, ["rr", "kb%d" % i], ["z%d" % i])
-        quant("zq", 0, 128, T.tt[:, 0:512], ["z0", "z1", "z2", "ts3"], ["zq"])
-        mm(4, "zq", 0, "jq", 0, C, True, True, ["zq", "jq"])
-        ts(col(HH), col(JB), 0.5 - 1.0 / 2048, 0.25, A.mult, A.add, ["jb"], ["hh"])
-        ts(col(UU), col(JB), 0.5, 0.5, A.mult, A.add, ["jb"], ["uc"])
-        digits(1, JB, T1, "jb", "w3")
+                places(i)
+            best_place(0)
+        mm(3, pat, 0, tab, 0, C, True, True, tall + pkeys)
+        best_place(1)
+        best_place(2)
+        scan(T.pr[:], bank(3, C), T.one[:, 0:C], -1e29, A.max, A.mult, ["one"], ["pr"], (3,))
+        act(T.dz[:, 1:C], T.pr[:, 0:C - 1], F.Sign, -1.0, T.pr[:, C - 1:C], ["pr"], ["dz", "jb"], accum=col(JB))
+        steps = ["th0v", "th1v", "th2v", "th1", "th3"]
+        for n in range(2):
+            quant("zq", 128 * n, 128, T.th[:, 4 * n:4 * n + 512], steps, ["zq%d" % n])
+            mm(4, "zq", 128 * n, "jq", 0, C, n == 0, n == 1, ["zq%d" % n, "jq"])
+        if t == 0:
+            later_constants()
+        rounded(JB, T1, "jb", "w3")
+        act(T.ww[:, XA:XA + 256:2], T.rr[:], F.Relu, -1.0, col(JB), ["rr", "jb"], ["xa"])
+        act(col(HH), col(JB), F.Identity, 0.5, 0.375, ["jb"], ["hh"])
+        digits(W3, JB, T1, "jb", "w3")
+        if t == 0:
+            latch_constants()
         scan(T.la[:], T.dz[:], bank(4, C), 1e4, A.add, A.min, ["dz", "dz0"], ["la"], (4,))
         f = T.la[:, C - 1:C]
-        ts(slot("tt", 1, 0), T.kk[:], col(HH), f, A.add, A.is_ge, ["kk", "hh", "la"], ["t2s0"])
-        act(slot("tt", 1, 1), T.neg[:], F.Identity, f, col(UU), ["neg", "uc", "la"], ["t2s1"])
-        quant("t2q", 0, 128, T.tt[:, 512:1024], ["t2s0", "t2s1", "t2s2", "ts3"], ["t2q"])
+        ts(T.ww[:, 0:512:2], T.ww[:, XA:XA + 256], col(HH), f, A.add, A.is_equal, ["xa", "xaz", "hh", "la"], ["t2s"])
+        quant("t2q", 0, 128, tile(T2), ["t2s", "z13"], ["t2q"])
         mm(5, "t2q", 0, "w2q", 0, 128, True, True, ["t2q", "w2q"])
-        for s in (1, 2):
-            act(slot("tt", 2, s), T.ni[:], F.Relu, f, col(UU), ["ni", "uc", "la"], ["t3s%d" % s])
-        quant("w3q", 0, 128, T.ww[:, 512:1024], ["ws0", "ws3", "w31", "w32"], ["w3q"])
-        note(pl, "v", lambda: V.tensor_tensor(slot("tt", 2, 0), bank(5), T.nd[:], A.is_gt), ["nd"], ["t3s0"], (5,))
-        quant("t3q", 0, 128, T.tt[:, 1024:1536], ["t3s0", "t3s1", "t3s2", "ts3"], ["t3q"])
+        ts(T.ww[:, 512 * T3 + 1:512 * T3 + 512:2], T.xd[:], col(HH), f, A.add, A.is_equal, ["xd", "hh", "la"], ["t3s"])
+        quant("w3q", 0, 128, tile(W3), ["ws0", "z2", "w31", "w32"], ["w3q"])
+        note(pl, "v", lambda: V.tensor_tensor(slot("ww", T3, 0), bank(5), T.dd[:], A.is_lt), ["dd"], ["t3s0"], (5,))
+        quant("t3q", 0, 128, tile(T3), ["t3s0", "t3s", "z2"], ["t3q"])
         mm(6, "w3q", 0, "t3q", 0, 128, True, True, ["w3q", "t3q"])
+        if t == 0:
+            quant("w4q", 0, 128, tile(W4), ["ws0", "z2", "w41", "w42"], ["w4q"])
+            quant_e(0)
+        mm(7, "w4q", 0, "t3q", 0, 128, True, True, ["w4q", "t3q"])
+        act(T.val[:], bank(7), F.Copy, 1.0, 0.0, (), ["val"], (7,))
         scan(T.sel[:], T.cs[:], bank(6), 0.0, A.add, A.max, ["cs"], ["sel"], (6,))
-        ts(T[off][:], T.sel[:, 15:128:16], col(CORR), 4.0, A.subtract, A.mult, ["sel", "corr"], [off])
+        ts(T[off][:], T.sel[:, 15:128:16], col(CORR), None, A.subtract, None, ["sel", "corr"], [off])
         pick(pk, 0, 128, tab, C, off, tall + [off], pk)
         own = [pk + "c", pk + "s"]
 
         dsts = [r for r in summers if r != rank]
         if dsts:
-            a = 128 * rank
-            write(T[pk][:].bitcast(u8), T[land][:, a:a + 128].bitcast(u8), dsts, "ar%d" % rank, [pk + "c"])
-            write(T[pk + "s"][:], T[land + "s"][:, a:a + 128], dsts, "ar%d" % rank, [pk + "s"])
+            send(pk, land, 128 * rank, dsts, "ar%d" % rank, own, t == 0)
 
-        act(T.pas[0:1, 128 * t:128 * t + 128], T.ps[0:1, 3072:3200], F.Copy, 4.0, 0.0, (), ["pas%d" % t], (6,))
         if t == 0:
-            digits(2, V4, T4, "v4", "w4")
-            for b in range(4):
-                quant("eq", 128 * b, 128, T.uu[:, 3 - b:515 - b], ["uu"], ["e%d" % b])
-            quant("w4q", 0, 128, T.ww[:, 1024:1536], ["ws0", "ws3", "w41", "w42"], ["w4q"])
-        mm(7, "w4q", 0, "t3q", 0, 128, True, True, ["w4q", "t3q"])
-        act(T.val[:], bank(7), F.Copy, 4.0, 0.0, (), ["val"], (7,))
+            iota(T.tl[:, C:2 * C], [[1, C]], 0, 0, ["tl1"])
+
+        def list_out(t=t):
+            act(T.pas[0:1, 128 * t:128 * t + 128], T.ps[0:1, 3072:3200], F.Copy, 1.0, 0.0, (), ["pas%d" % t], (6,))
 
         def table_list(t=t, off=off, tof=tof):
             win = T.tl[:, C * t:C * t + C]
             note(pl, "v", lambda: V.tensor_copy(win.indirect(T[off][:]), T.val[:]), ["val", off], ["tl%d" % t])
+
+        def table_offsets(t=t, tof=tof):
             for i in range(3):
                 scan(T.selt[:, 128 * i:128 * i + 128], T.cs[:], T.tl[:, C * t + 128 * i:C * t + 128 * i + 128], 0.0,
                      A.add, A.max, ["cs", "tl%d" % t], ["selt%d" % i])
             ts(T[tof][:], T.selt[:, 15:C:16], col(CORR), None, A.subtract, None,
                ["selt0", "selt1", "selt2", "corr"], [tof])
 
-        def held(pk=pk, own=own):
+        late = t == 1 and rank == LAST
+        vb = 0 if late else 4
+
+        def held(pk=pk, own=own, vb=vb):
             for b in range(4):
-                mm(4 + b, "eq", 128 * b, pk, 0, 128, True, False, ["e%d" % b] + own)
+                mm(vb + b, "eq", 128 * b, pk, 0, 128, True, False, ["e%d" % b] + own)
 
         def evacuate(first, tile, c, name):
             for b in range(4):
-                if b % 2 == 0:
+                if b % 2 == 1:
                     ts(slot(tile, 0, b), bank(first + b), c, None, A.mult, None, (), [name + str(b)], (first + b,))
                 else:
                     act(slot(tile, 0, b), bank(first + b), F.Copy, c, 0.0, (), [name + str(b)], (first + b,))
             return [name + str(b) for b in range(4)]
 
-        late = t == 1 and rank == LAST
         if not late:
+            list_out()
             table_list()
+            if t == 0:
+                for b in range(1, 4):
+                    quant_e(b)
+            table_offsets()
             held()
             if (t == 0) == (rank == LAST):
                 quant_w()
@@ -340,7 +388,7 @@ def rank_program(g, core, T, topo):
                 if r == rank:
                     mv, a, keys = pk, 0, own
                 else:
-                    arrives("land%d" % r, "ar%d" % r, 2 * lanes(r, [d for d in summers if d != r])[1])
+                    arrives("land%d" % r, "ar%d" % r, r, [d for d in summers if d != r], t == 0)
                     mv, a, keys = land, 128 * r, ["land%d" % r]
                 for b in range(4):
                     mm(b, "eq", 128 * b, mv, a, 128, n == 0, n == N - 1, ["e%d" % b] + keys)
@@ -351,49 +399,60 @@ def rank_program(g, core, T, topo):
         far = "b1l" if t == 0 else "b2l"
         giver = min(summers, key=lambda r: (topo.die(cores[r]) != topo.die(cores[others[0]]), -r))
         if rank == giver:
-            write(T[pat][:].bitcast(u8), T[far][:].bitcast(u8), others, "arb", pkeys)
-            write(T[pat + "s"][:], T[far + "s"][:], others, "arb", pkeys)
+            send(pat, far, 0, others, "arb", pkeys, False)
         if rank in others:
             pat, pkeys = far, [far]
-            arrives(far, "arb", 2 * lanes(giver, others)[1])
-        if t == 1:
-            arrives("sent", "sent", pl["n"]["sent"])
-            dma("y", T.pa[:], T.pas[0:1, :], ["pas0", "pas1", "sent"], (), "out")
+            arrives(far, "arb", giver, others, False)
         if late:
+            list_out()
             held()
             table_list()
+        if t == 1 and not late:
+            dma("y", T.pa[:], T.pas[0:1, :], ["pas0", "pas1"], (), "out")
 
         for b in range(4):
-            mm(4 + b, "eq", 128 * b, pat, 0, 128, False, True, ["e%d" % b] + pkeys)
+            mm(vb + b, "eq", 128 * b, pat, 0, 128, False, True, ["e%d" % b] + pkeys)
         if t == 1:
             for o in range(2):
-                mm(o, "wq", 128 * o, pat, 0, 128, True, True, ["wq"] + pkeys)
-        quant(tab, C, 128, T.vt[:], evacuate(4, "vt", 0.5, "vt"), ["v%d" % t])
+                mm(4 - vb + o, "wq", 128 * o, pat, 0, 128, True, True, ["wq"] + pkeys)
+        keys = evacuate(vb, "vt", 0.5, "vt")
+        if late:
+            table_offsets()
+        quant(tab, C, 128, T.vt[:], keys, ["v%d" % t])
         if t == 0:
             pick("wb", 0, 256, "wa", 512, tof, tall + ["v0", tof], "t1a")
             pick("wb", 256, 128, "wa", 512, tof, tall + ["v0", tof], "t1b")
             tkeys = [["t1ac", "t1as"], ["t1ac", "t1as"], ["t1bc", "t1bs"]]
 
-    for o in range(2):
-        a = 512 * o + C
-        act(T.ysb[:, a:a + 128], bank(o), F.Copy, 1.0, 0.0, (), ["yb%d" % o], (o,))
-        dma("y", T.y[:, a:a + 128], T.ysb[:, a:a + 128], ["yb%d" % o], (), "out")
+    def copy(a, n, b, key):
+        note(pl, "v", lambda: V.tensor_copy(T.ysb[:, a:a + n], bank(b, n)), (), [key], (b,))
+
+    early = rank != LAST
+    act(T.ysb[:, C:512], bank(4 - vb), F.Copy, 1.0, 0.0, (), ["yb0"], (4 - vb,))
+    if early:
+        dma("y", T.y[:, C:512], T.ysb[:, C:512], ["yb0"], (), "out")
     H = C // 2
     for h in range(2):
         pick("tc", H * h, H, "wb", 512, "tof2", tall + ["v1", "tof2"], "t2%d" % h)
+    copy(512 + C, 128, 5 - vb, "yb1")
     for h in range(2):
         for o in range(2):
-            mm(2 + 2 * h + o, "wq", 128 * o, "tc", H * h, H, True, True, ["wq", "t2%dc" % h, "t2%ds" % h])
+            mm(vb + 2 * h + o, "wq", 128 * (1 - o), "tc", H * h, H, True, True, ["wq", "t2%dc" % h, "t2%ds" % h])
     dma("y", T.oc[:], T.tc[:].bitcast(u8), ["t20c", "t21c"], (), "out")
-    for k in range(2):
-        dma("y", T.osc[4 * k:4 * k + 4, :], T.tcs[32 * k:32 * k + 4, :], ["t20s", "t21s"], (), "out")
+    apart = early and OPT["tail"] == 0
+    if apart:
+        dma("y", T.y[:, 512 + C:1024], T.ysb[:, 512 + C:1024], ["yb1"], (), "out")
+    if not early:
+        dma("y", T.pa[:], T.pas[0:1, :], ["pas0", "pas1"], (), "out")
     for h in range(2):
-        b = 2 + 2 * h
-        note(pl, "v", lambda b=b, h=h: V.tensor_copy(T.ysb[:, H * h:H * h + H], bank(b, H)), (), ["y0%d" % h], (b,))
-        act(T.ysb[:, 512 + H * h:512 + H * h + H], bank(b + 1, H), F.Copy, 1.0, 0.0, (), ["y1%d" % h], (b + 1,))
-    dma("y", T.y[:, 0:C], T.ysb[:, 0:C], ["y00", "y01"], (), "out")
-    dma("s", T.y[:, 512:512 + C], T.ysb[:, 512:512 + C], ["y10", "y11", "sent"], (), "out")
-    for k in range(2, 4):
-        dma("s", T.osc[4 * k:4 * k + 4, :], T.tcs[32 * k:32 * k + 4, :], ["t20s", "t21s"], (), "out")
+        b = vb + 2 * h
+        act(T.ysb[:, 512 + H * h:512 + H * h + H], bank(b, H), F.Copy, 1.0, 0.0, (), ["y1%d" % h], (b,))
+        copy(H * h, H, b + 1, "y0%d" % h)
+    n = C if early else 512
+    dma("y", T.y[:, 0:n], T.ysb[:, 0:n], ["y00", "y01", "yb0"], (), "out")
+    n = C if apart else 512
+    dma("s", T.y[:, 512:512 + n], T.ysb[:, 512:512 + n], ["y10", "y11", "yb1"], (), "out")
+    for k in range(4):
+        dma("ys"[k % 2], T.osc[4 * k:4 * k + 4, :], T.tcs[32 * k:32 * k + 4, :], ["t20s", "t21s"], (), "out")
 
     emit(pl, queues, T, [("g", "sent"), ("y", "out")])

@@ -5,25 +5,26 @@ C = 384
 N = 4
 LAST = N - 1
 BIG = 1.5 * 2.0 ** 28
-OPT = {"w1": 1, "load": 1, "tail": 0}
+OPT = {"w1": 1, "once": -1, "pieces": 1, "load": 0, "H": 160, "cut": 96}
 
 SCRATCH = {"ps": ("psum", [128, 4096], "float32")}
 for _n, _w in (("xt", 1536), ("bt", 512), ("wt", 1024), ("rr", 128), ("fm", 128), ("dd", 128),
-               ("one", 516), ("uu", 516), ("jt", 1536), ("th", 516),
-               ("xd", 256), ("ww", 2816), ("at", 512), ("vt", 512), ("dz", 384), ("sg", 128)):
+               ("one", 516), ("uu", 516), ("jt", 1536), ("th", 516), ("tv", 516), ("qt", 516),
+               ("xd", 256), ("xa", 128), ("ww", 2560), ("at", 512), ("vt", 512), ("dz", 384), ("sg", 128)):
     SCRATCH[_n] = ("sbuf", [128, _w], "bfloat16")
-for _n, _w in (("pc", 384), ("pr", 384), ("la", 384), ("sel", 128), ("cs", 128), ("tl", 768), ("val", 128),
+for _n, _w in (("pc", 512), ("pr", 384), ("la", 384), ("sel", 128), ("cs", 128), ("tl", 768), ("val", 128), ("vr", 128),
                ("selt", 384), ("cl", 32), ("pas", 256), ("ysb", 1024)):
     SCRATCH[_n] = ("sbuf", [128, _w], "float32")
 for _n, _w in (("wa", 512), ("wb", 512), ("tc", 384), ("b0", 128), ("b1q", 128), ("b1l", 128), ("b2q", 128),
-               ("b2l", 128), ("p1", 128), ("p2", 128), ("l1", 512), ("l2", 512), ("jq", 384), ("eq", 512),
-               ("zq", 256), ("t2q", 128), ("t3q", 128), ("w2q", 128), ("w3q", 128), ("w4q", 128), ("wq", 256)):
+               ("b2l", 128), ("p1", 128), ("p2", 128), ("l1", 512), ("l2", 512), ("l3", 512), ("jq", 512), ("eq", 512),
+               ("zq", 256), ("t2q", 128), ("t3q", 128), ("w2q", 128), ("w3q", 128), ("w4q", 128), ("wq", 256),
+               ("j1", 384), ("rq", 384)):
     SCRATCH[_n] = ("sbuf", [128, _w], "float8_e4m3fn_x4")
     SCRATCH[_n + "s"] = ("sbuf", [128, _w], "uint8")
 for _n, _w in (("off1", 8), ("off2", 8), ("tof1", 24), ("tof2", 24)):
     SCRATCH[_n] = ("sbuf", [128, _w], "uint16")
 
-SEMAPHORES = ["cv", "cs", "cp", "cg", "db", "dx0", "dx1", "dx2", "dw", "out", "sent",
+SEMAPHORES = ["cv", "cs", "cp", "cg", "db", "dx0", "dx1", "dx2", "dw", "out", "outg", "sent",
               "ar0", "ar1", "ar2", "ar3", "arb"]
 COUNTER = {"v": "cv", "s": "cs", "p": "cp", "g": "cg"}
 
@@ -114,12 +115,12 @@ def rank_program(g, core, T, topo):
 
     def col(i):
         return T.cl[:, i:i + 1]
-    JB, HH, T1, P2, Q32, NPM, CORR, V4, T4 = range(9)
+    JB, HH, T1, P2, Q32, NPM, CORR, LIM = range(8)
 
     def slot(buf, piece, t, pieces=1):
         return T[buf][:, 512 * piece + t:512 * (piece + pieces):4]
 
-    T2, W2, W3, W4, T3, XA = 0, 1, 2, 3, 4, 2560
+    T2, W2, W3, W4, T3 = range(5)
 
     def tile(piece):
         return T.ww[:, 512 * piece:512 * piece + 512]
@@ -149,8 +150,8 @@ def rank_program(g, core, T, topo):
         note(pl, "p", lambda: P.matmul_mx(bank(b, n), T[st][:, sa:sa + 128], T[st + "s"][:, sa:sa + 128],
                                           T[mv][:, ma:ma + n], T[mv + "s"][:, ma:ma + n], start, stop), r, (), (b,))
 
-    def pick(dst, a, n, win, wn, off, r, w):
-        o = T[off][:, a // 16:(a + n) // 16]
+    def pick(dst, a, n, win, wn, off, r, w, first=0):
+        o = T[off][:, (a - first) // 16:(a - first + n) // 16]
         note(pl, "v", lambda: V.tensor_copy(T[dst][:, a:a + n].bitcast(u32),
                                             T[win][:, 0:wn].bitcast(u32).indirect(o)), r, [w + "c"])
         note(pl, "s", lambda: S.activation(T[dst + "s"][:, a:a + n], T[win + "s"][:, 0:wn].indirect(o), F.Copy),
@@ -173,17 +174,31 @@ def rank_program(g, core, T, topo):
                                dsts=[dst for d in dsts])
         note(pl, "g", lambda: g.remote_dma_fused([tr], local_sem=T.sem.sent), r, (), sem="sent", inc=n)
 
+    def send_once(name, land, dsts, sem, keys):
+        ids = [DstId(rid=topo.addr(cores[d])[0], pnc=topo.addr(cores[d])[1]) for d in dsts]
+        sides = [(T[name][:, C:512].bitcast(u8), T[land][:, C:512].bitcast(u8)), (T[name + "s"][:], T[land + "s"][:])]
+        trs = [RemoteDMATransfer(dst_ids=ids, dma_engine_mask=lanes(rank, dsts, part)[0], remote_sem=T.sem[sem],
+                                 src=src, dsts=[dst for d in dsts]) for part, (src, dst) in enumerate(sides)]
+        note(pl, "g", lambda: g.remote_dma_fused(trs, local_sem=T.sem.sent), keys, (), sem="sent",
+             inc=lanes(rank, dsts)[1])
+
     def calls(src, dsts, first):
         if first and OPT["w1"] == 1:
             return [(0, dsts, 0), (1, dsts, 1)]
         if first and OPT["w1"] == 2:
             return [(0, dsts[:2], 0), (1, dsts, 1)] + ([(0, dsts[2:], 1)] if dsts[2:] else [])
+        if first and OPT["w1"] == 4:
+            later = [(0, [2], 1)] if 2 in dsts else []
+            return [(0, [d for d in dsts if d != 2], 0), (1, dsts, 1)] + later
+        if first and OPT["w1"] == 3:
+            return [(0, dsts[:1], 0), (0, dsts[1:2], 1), (1, dsts, None)] + ([(0, dsts[2:], None)] if dsts[2:] else [])
         return [(0, dsts, None), (1, dsts, None)]
 
     def send(name, land, a, dsts, sem, keys, first):
         for kind, ds, part in calls(rank, dsts, first):
-            if kind == 0:
-                write(T[name][:].bitcast(u8), T[land][:, a:a + 128].bitcast(u8), ds, sem, keys[:1], part)
+            if kind != 1:
+                c, d = {0: (0, 128), 2: (0, OPT["cut"]), 3: (OPT["cut"], 128)}[kind]
+                write(T[name][:, c:d].bitcast(u8), T[land][:, a + c:a + d].bitcast(u8), ds, sem, keys[:1], part)
             else:
                 write(T[name + "s"][:], T[land + "s"][:, a:a + 128], ds, sem, keys[-1:], part)
 
@@ -193,13 +208,13 @@ def rank_program(g, core, T, topo):
 
     if OPT["load"] == 0:
         dma("y", T.bt[:], T.b[:], (), ["bt"], "db")
-        dma("s", T.xt[:, 0:1024], T.x[:, 0:1024], (), ["xt0", "xt1"], "dx0")
+        dma("y", T.xt[:, 0:1024], T.x[:, 0:1024], (), ["xt0", "xt1"], "dx0")
         dma("y", T.xt[:, 1024:1536], T.x[:, 1024:1536], (), ["xt2"], "dx2")
     else:
         dma("y", T.bt[:], T.b[:], (), ["bt"], "db")
         dma("s", T.xt[:, 0:512], T.x[:, 0:512], (), ["xt0"], "dx0")
         dma("y", T.xt[:, 512:1024], T.x[:, 512:1024], (), ["xt1"], "dx1")
-        dma("s", T.xt[:, 1024:1536], T.x[:, 1024:1536], (), ["xt2"], "dx2")
+        dma("y", T.xt[:, 1024:1536], T.x[:, 1024:1536], (), ["xt2"], "dx2")
     dma("y", T.wt[:], T.w[:], ["xt1", "xt2"], ["wt"], "dw")
 
     def iota(out, pat, base, cm, w):
@@ -213,7 +228,6 @@ def rank_program(g, core, T, topo):
 
     fill(T.one[:], 1.0, ["one"])
     iota(T.dd[:], [[1, 128]], 0, -1, ["dd"])
-    iota(col(V4), [[1, 1]], C, 1, ["v4"])
     iota(col(P2), [[1, 1]], -15, 2, ["p2c"])
     iota(T.rr[:], [[1, 128]], 0, 0, ["rr"])
 
@@ -223,25 +237,25 @@ def rank_program(g, core, T, topo):
     const(slot("jt", 2, 1), 128, 0.0, ["jz3"])
     const(T.th[:, 3:516:4], 129, 0.25, ["th3"])
     for i in range(3):
-        ts(slot("jt", i, i), T.dd[:], 0.0, -0.125, A.is_equal, A.mult, ["dd"], ["ji%d" % i])
+        ts(slot("jt", i, i), T.dd[:], 0.0, 0.25, A.is_equal, A.mult, ["dd"], ["ji%d" % i])
         ts(slot("jt", i, 3), T.dd[:], 0.0, float(i), A.is_ge, A.add, ["dd"], ["jn%d" % i])
     sel_g(slot("ww", W2, 2), slot("jt", 0, 3), [[1, 128]], A.not_equal, 256.0, 0, -1, ["jn0"], ["w2s2"])
     iota(T.xd[:], [[1, 128], [0, 2]], 0, -1, ["xd"])
     iota(T.fm[:], [[0, 8], [2, 16]], -15, 0, ["fm"])
-    sel_g(T.uu[:], T.one[:], [[1, 516]], A.is_equal, 0.0, -3, -4, ["one"], ["uu"])
-    fill(T.th[:, 0:3], 1.0, ["th1"])
-    quant("jq", 0, C, T.jt[:], ["jz0", "jz1", "jz2", "jz3", "ji0", "ji1", "ji2", "jn0", "jn1", "jn2"], ["jq"])
+    const(T.qt[:], 516, 0.25, ["qt"])
+    sel_g(T.uu[:], T.qt[:], [[1, 516]], A.is_equal, 0.0, -3, -4, ["qt"], ["uu"])
+    fill(T.th[:, 0:3], 1.0, ["th"])
     const(T.dz[:, 0:1], 1, 0.0, ["dz0"])
-    const(slot("ww", W2, 0), 128, -1.0, ["w2s0"])
-    const(T.ww[:, 1:1024:2], 512, 0.0, ["z13"])
-    const(T.ww[:, XA + 1:XA + 256:2], 128, 0.0, ["xaz"])
+    const(slot("ww", W2, 0), 128, 0.25, ["w2s0"])
+    const(T.ww[:, 513:1024:2], 256, 0.0, ["w2z"])
     const(slot("ww", W3, 0, 2), 256, 1.0, ["ws0"])
-    const(slot("ww", W3, 2, 3), C, 0.0, ["z2"])
+    iota(T.vr[:], [[1, 128]], C, 0, ["vr"])
     iota(T.tl[:, 0:C], [[1, C]], 0, 0, ["tl0"])
 
     def later_constants():
-        quant("w2q", 0, 128, tile(W2), ["w2s0", "z13", "w2s2"], ["w2q"])
+        quant("w2q", 0, 128, tile(W2), ["w2s0", "w2z", "w2s2"], ["w2q"])
         ts(col(Q32), col(P2), BIG, -BIG, A.add, A.add, ["p2c"], ["q32"])
+        fill(slot("ww", W3, 2, 3), 0.0, ["z2"])
         ts(col(NPM), col(P2), -1.0, col(Q32), A.mult, A.add, ["q32", "p2c"], ["npm"])
 
     def latch_constants():
@@ -256,8 +270,8 @@ def rank_program(g, core, T, topo):
         act(slot("ww", piece, 1), T.one[:, 0:128], F.Identity, -BIG, col(t), ["one", name + "t"], [name + "1"])
         act(slot("ww", piece, 3), slot("ww", piece, 1), F.Identity, -1.0, col(value), [name + "1", key], [name + "2"])
 
-    rounded(V4, T4, "v4", "w4")
-    digits(W4, V4, T4, "v4", "w4")
+    def copy(a, n, b, key):
+        note(pl, "v", lambda: V.tensor_copy(T.ysb[:, a:a + n], bank(b, n)), (), [key], (b,))
 
     def quant_e(b):
         quant("eq", 128 * b, 128, T.uu[:, 3 - b:515 - b], ["uu"], ["e%d" % b])
@@ -268,11 +282,13 @@ def rank_program(g, core, T, topo):
     def quant_w():
         quant("wq", 0, 256, T.wt[:], ["wt"], ["wq"])
 
-    def best_place(i):
+    def running(i, b):
+        scan(T.pc[:, 128 * i:128 * i + 128], bank(b), T.one[:, 0:128], -1e29, A.max, A.mult, ["one"], ["pc%d" % i], (b,))
+
+    def step(buf, i):
         a = 128 * i
-        scan(T.pc[:, a:a + 128], bank(i), T.one[:, 0:128], -1e29, A.max, A.mult, ["one"], ["pc%d" % i], (i,))
-        act(T.th[:, 4 + i:516:4], T.pc[:, a:a + 128], F.Sign, -1.0, T.pc[:, a + 127:a + 128], ["pc%d" % i],
-            ["th%dv" % i])
+        act(T[buf][:, 4 + i:516:4], T.pc[:, a:a + 128], F.Sign, -1.0, T.pc[:, a + 127:a + 128], ["pc%d" % i],
+            [buf + str(i)])
 
     pat, pkeys = "b0", ["b0"]
     tkeys = [["t0p0"], ["t0p1"], ["t0p2"]]
@@ -287,60 +303,75 @@ def rank_program(g, core, T, topo):
 
         if t == 0:
             quant("b0", 0, 128, T.bt[:], ["bt"], ["b0"])
+            quant("jq", 0, C, T.jt[:], ["jz0", "jz1", "jz2", "jz3", "ji0", "ji1", "ji2", "jn0", "jn1", "jn2"], ["jq"])
             quant_x(0)
             places(0)
             quant_x(1)
             places(1)
-            best_place(0)
             quant_x(2)
             places(2)
-        else:
+            mm(3, pat, 0, tab, 0, C, True, True, tall + pkeys)
             for i in range(3):
-                places(i)
-            best_place(0)
-        mm(3, pat, 0, tab, 0, C, True, True, tall + pkeys)
-        best_place(1)
-        best_place(2)
-        scan(T.pr[:], bank(3, C), T.one[:, 0:C], -1e29, A.max, A.mult, ["one"], ["pr"], (3,))
+                running(i, i)
+                step("th", i)
+        gb, zb = (3, 4) if t == 0 else (5, 3)
+        scan(T.pr[:], bank(gb, C), T.one[:, 0:C], -1e29, A.max, A.mult, ["one"], ["pr"], (gb,))
         act(T.dz[:, 1:C], T.pr[:, 0:C - 1], F.Sign, -1.0, T.pr[:, C - 1:C], ["pr"], ["dz", "jb"], accum=col(JB))
-        steps = ["th0v", "th1v", "th2v", "th1", "th3"]
+        buf, turn, keys = ("th", "jq", ["jq"]) if t == 0 else ("tv", "j1", ["j0c", "j0s", "j1c", "j1s"])
         for n in range(2):
-            quant("zq", 128 * n, 128, T.th[:, 4 * n:4 * n + 512], steps, ["zq%d" % n])
-            mm(4, "zq", 128 * n, "jq", 0, C, n == 0, n == 1, ["zq%d" % n, "jq"])
+            quant("zq", 128 * n, 128, T[buf][:, 4 * n:4 * n + 512], [buf + str(i) for i in range(4)] + [buf], ["zq%d" % n])
+            mm(zb, "zq", 128 * n, turn, 0, C, t == 0 and n == 0, n == 1, ["zq%d" % n] + keys)
         if t == 0:
             later_constants()
         rounded(JB, T1, "jb", "w3")
-        act(T.ww[:, XA:XA + 256:2], T.rr[:], F.Relu, -1.0, col(JB), ["rr", "jb"], ["xa"])
-        act(col(HH), col(JB), F.Identity, 0.5, 0.375, ["jb"], ["hh"])
-        digits(W3, JB, T1, "jb", "w3")
+        act(T.xa[:], T.rr[:], F.Relu, -1.0, col(JB), ["rr", "jb"], ["xa"])
+        act(col(HH), col(JB), F.Identity, -0.5, -0.75, ["jb"], ["hh"])
         if t == 0:
-            latch_constants()
-        scan(T.la[:], T.dz[:], bank(4, C), 1e4, A.add, A.min, ["dz", "dz0"], ["la"], (4,))
+            const(T.ww[:, 1:512:2], 256, 0.0, ["z13"])
+        act(slot("ww", W3, 1), T.one[:, 0:128], F.Identity, -BIG, col(T1), ["one", "w3t"], ["w31"])
+        scan(T.la[:], T.dz[:], bank(zb, C), 1e4, A.add, A.min, ["dz", "dz0"], ["la"], (zb,))
         f = T.la[:, C - 1:C]
-        ts(T.ww[:, 0:512:2], T.ww[:, XA:XA + 256], col(HH), f, A.add, A.is_equal, ["xa", "xaz", "hh", "la"], ["t2s"])
-        quant("t2q", 0, 128, tile(T2), ["t2s", "z13"], ["t2q"])
+        ts(slot("ww", T2, 0), T.xa[:], col(HH), f, A.subtract, A.is_equal, ["xa", "hh", "la"], ["t2s0"])
+        act(slot("ww", T2, 2), T.one[:, 0:128], F.Abs, f, col(HH), ["one", "hh", "la"], ["t2s2"])
+        act(slot("ww", W3, 3), slot("ww", W3, 1), F.Identity, -1.0, col(JB), ["w31", "jb"], ["w32"])
+        if t == 0:
+            act(col(LIM), col(P2), F.Identity, 0.125, 65.875, ["p2c"], ["lim"])
+            latch_constants()
+            const(slot("ww", W4, 1), 128, 512.0, ["w41"])
+            const(slot("ww", W4, 3), 128, 0.0, ["w42"])
+            for i in range(3):
+                const(slot("jt", i, i), 128, 0.0, ["ji%d" % i])
+            act(slot("jt", 0, 3, 3), slot("jt", 0, 3, 3), F.Copy, 2.0, 0.0, (), ["jn0", "jn1", "jn2"])
+        quant("t2q", 0, 128, tile(T2), ["t2s0", "t2s2", "z13"], ["t2q"])
         mm(5, "t2q", 0, "w2q", 0, 128, True, True, ["t2q", "w2q"])
-        ts(T.ww[:, 512 * T3 + 1:512 * T3 + 512:2], T.xd[:], col(HH), f, A.add, A.is_equal, ["xd", "hh", "la"], ["t3s"])
+        ts(T.ww[:, 512 * T3 + 1:512 * T3 + 512:2], T.xd[:], col(HH), f, A.subtract, A.is_equal, ["xd", "hh", "la"],
+           ["t3s"])
         quant("w3q", 0, 128, tile(W3), ["ws0", "z2", "w31", "w32"], ["w3q"])
-        note(pl, "v", lambda: V.tensor_tensor(slot("ww", T3, 0), bank(5), T.dd[:], A.is_lt), ["dd"], ["t3s0"], (5,))
+        ts(slot("ww", T3, 0), bank(5), col(LIM), None, A.is_gt, None, ["lim"], ["t3s0"], (5,))
         quant("t3q", 0, 128, tile(T3), ["t3s0", "t3s", "z2"], ["t3q"])
         mm(6, "w3q", 0, "t3q", 0, 128, True, True, ["w3q", "t3q"])
         if t == 0:
             quant("w4q", 0, 128, tile(W4), ["ws0", "z2", "w41", "w42"], ["w4q"])
             quant_e(0)
         mm(7, "w4q", 0, "t3q", 0, 128, True, True, ["w4q", "t3q"])
-        act(T.val[:], bank(7), F.Copy, 1.0, 0.0, (), ["val"], (7,))
         scan(T.sel[:], T.cs[:], bank(6), 0.0, A.add, A.max, ["cs"], ["sel"], (6,))
         ts(T[off][:], T.sel[:, 15:128:16], col(CORR), None, A.subtract, None, ["sel", "corr"], [off])
-        pick(pk, 0, 128, tab, C, off, tall + [off], pk)
+        once = t == 1 and rank == OPT["once"]
         own = [pk + "c", pk + "s"]
+        pk, pa = ("jq", C) if once else (pk, 0)
+        pick(pk, pa, 128, tab, C, off, tall + [off], own[0][:-1], pa)
 
         dsts = [r for r in summers if r != rank]
-        if dsts:
+        if once:
+            send_once(pk, "l3", dsts, "ar%d" % rank, own + ["jq"])
+        elif dsts:
             send(pk, land, 128 * rank, dsts, "ar%d" % rank, own, t == 0)
 
         if t == 0:
             iota(T.tl[:, C:2 * C], [[1, C]], 0, 0, ["tl1"])
+
+        def values():
+            note(pl, "v", lambda: V.tensor_tensor(T.val[:], bank(7), T.vr[:], A.min), ["vr"], ["val"], (7,))
 
         def list_out(t=t):
             act(T.pas[0:1, 128 * t:128 * t + 128], T.ps[0:1, 3072:3200], F.Copy, 1.0, 0.0, (), ["pas%d" % t], (6,))
@@ -359,9 +390,9 @@ def rank_program(g, core, T, topo):
         late = t == 1 and rank == LAST
         vb = 0 if late else 4
 
-        def held(pk=pk, own=own, vb=vb):
+        def held(pk=pk, pa=pa, own=own, vb=vb):
             for b in range(4):
-                mm(vb + b, "eq", 128 * b, pk, 0, 128, True, False, ["e%d" % b] + own)
+                mm(vb + b, "eq", 128 * b, pk, pa, 128, True, False, ["e%d" % b] + own)
 
         def evacuate(first, tile, c, name):
             for b in range(4):
@@ -373,12 +404,19 @@ def rank_program(g, core, T, topo):
 
         if not late:
             list_out()
+            values()
+            if t == 0:
+                quant_e(1)
+                quant_e(2)
             table_list()
             if t == 0:
-                for b in range(1, 4):
-                    quant_e(b)
+                quant_e(3)
             table_offsets()
             held()
+            if t == 0:
+                quant("rq", 0, C, T.jt[:], ["ji0", "ji1", "ji2", "jn0"], ["rq"])
+                const(T.tv[:, 0:4], 4, 1.0, ["tv"])
+                pick("j1", 0, C // 2, "eq", 512, tof, ["e0", "e1", "e2", "e3", tof], "j0")
             if (t == 0) == (rank == LAST):
                 quant_w()
 
@@ -390,10 +428,13 @@ def rank_program(g, core, T, topo):
                 else:
                     arrives("land%d" % r, "ar%d" % r, r, [d for d in summers if d != r], t == 0)
                     mv, a, keys = land, 128 * r, ["land%d" % r]
+                    if t == 1 and r == OPT["once"]:
+                        mv, a = "l3", C
+                        pl["wr"][keys[0]] = ("d", "ar%d" % r, lanes(r, [rank])[1])
                 for b in range(4):
                     mm(b, "eq", 128 * b, mv, a, 128, n == 0, n == N - 1, ["e%d" % b] + keys)
             pat = "b1q" if t == 0 else "b2q"
-            quant(pat, 0, 128, T.at[:], evacuate(0, "at", 0.25, "at"), [pat])
+            quant(pat, 0, 128, T.at[:], evacuate(0, "at", 1.0, "at"), [pat])
             pkeys = [pat]
         others = [r for r in range(N) if r not in summers]
         far = "b1l" if t == 0 else "b2l"
@@ -403,56 +444,76 @@ def rank_program(g, core, T, topo):
         if rank in others:
             pat, pkeys = far, [far]
             arrives(far, "arb", giver, others, False)
+        if t == 0:
+            pick("j1", C // 2, C // 2, "eq", 512, tof, ["e0", "e1", "e2", "e3", tof], "j1")
         if late:
             list_out()
+            values()
             held()
             table_list()
         if t == 1 and not late:
             dma("y", T.pa[:], T.pas[0:1, :], ["pas0", "pas1"], (), "out")
 
+        if t == 0:
+            mm(3, "zq", 0, "rq", 0, C, True, False, ["rq", "zq0"])
         for b in range(4):
             mm(vb + b, "eq", 128 * b, pat, 0, 128, False, True, ["e%d" % b] + pkeys)
         if t == 1:
             for o in range(2):
-                mm(4 - vb + o, "wq", 128 * o, pat, 0, 128, True, True, ["wq"] + pkeys)
-        keys = evacuate(vb, "vt", 0.5, "vt")
+                mm(4 - vb + o, "wq", 128 * (1 - o), pat, 0, 128, True, True, ["wq"] + pkeys)
+        if t == 0:
+            for i in range(3):
+                mm(i, tab, 128 * i, pat, 0, 128, True, True, tkeys[i] + pkeys)
+        keys = evacuate(vb, "vt", 2.0, "vt")
+        if t == 0:
+            running(0, 0)
+        if t == 1:
+            act(T.ysb[:, 512 + C:1024], bank(4 - vb), F.Copy, 1.0, 0.0, (), ["yb1"], (4 - vb,))
         if late:
             table_offsets()
         quant(tab, C, 128, T.vt[:], keys, ["v%d" % t])
+        if t == 1:
+            copy(C, 128, 5 - vb, "yb0")
         if t == 0:
-            pick("wb", 0, 256, "wa", 512, tof, tall + ["v0", tof], "t1a")
-            pick("wb", 256, 128, "wa", 512, tof, tall + ["v0", tof], "t1b")
-            tkeys = [["t1ac", "t1as"], ["t1ac", "t1as"], ["t1bc", "t1bs"]]
+            mm(4, tab, C, pat, 0, 128, True, True, ["v0"] + pkeys)
+            running(1, 1)
+            pick("wb", 0, C, "wa", 512, tof, tall + ["v0", tof], "t1")
+            tkeys = [["t1c", "t1s"]] * 3
+            mm(5, pat, 0, "wb", 0, C, True, True, tkeys[0] + pkeys)
+            step("tv", 0)
+            step("tv", 1)
+            running(3, 4)
+            step("tv", 3)
+            running(2, 2)
+            step("tv", 2)
 
-    def copy(a, n, b, key):
-        note(pl, "v", lambda: V.tensor_copy(T.ysb[:, a:a + n], bank(b, n)), (), [key], (b,))
+    def scales_out(q, ks):
+        for k in ks:
+            dma(q, T.osc[4 * k:4 * k + 4, :], T.tcs[32 * k:32 * k + 4, :], ["t20s", "t21s"], (), "outg" if q == "g" else "out")
 
     early = rank != LAST
-    act(T.ysb[:, C:512], bank(4 - vb), F.Copy, 1.0, 0.0, (), ["yb0"], (4 - vb,))
     if early:
-        dma("y", T.y[:, C:512], T.ysb[:, C:512], ["yb0"], (), "out")
-    H = C // 2
-    for h in range(2):
-        pick("tc", H * h, H, "wb", 512, "tof2", tall + ["v1", "tof2"], "t2%d" % h)
-    copy(512 + C, 128, 5 - vb, "yb1")
-    for h in range(2):
+        for o in (1, 0):
+            dma("y", T.y[:, 512 * o + C:512 * o + 512], T.ysb[:, 512 * o + C:512 * o + 512], ["yb%d" % o], (), "out")
+    H = OPT["H"]
+    parts = ((0, H), (H, C - H))
+    for h, (a, n) in enumerate(parts):
+        pick("tc", a, n, "wb", 512, "tof2", tall + ["v1", "tof2"], "t2%d" % h)
         for o in range(2):
-            mm(vb + 2 * h + o, "wq", 128 * (1 - o), "tc", H * h, H, True, True, ["wq", "t2%dc" % h, "t2%ds" % h])
+            mm(vb + 2 * h + o, "wq", 128 * (1 - o), "tc", a, n, True, True, ["wq", "t2%dc" % h, "t2%ds" % h])
     dma("y", T.oc[:], T.tc[:].bitcast(u8), ["t20c", "t21c"], (), "out")
-    apart = early and OPT["tail"] == 0
-    if apart:
-        dma("y", T.y[:, 512 + C:1024], T.ysb[:, 512 + C:1024], ["yb1"], (), "out")
     if not early:
         dma("y", T.pa[:], T.pas[0:1, :], ["pas0", "pas1"], (), "out")
-    for h in range(2):
+    scales_out("y", range(4))
+    for h, (a, n) in enumerate(parts):
         b = vb + 2 * h
-        act(T.ysb[:, 512 + H * h:512 + H * h + H], bank(b, H), F.Copy, 1.0, 0.0, (), ["y1%d" % h], (b,))
-        copy(H * h, H, b + 1, "y0%d" % h)
-    n = C if early else 512
-    dma("y", T.y[:, 0:n], T.ysb[:, 0:n], ["y00", "y01", "yb0"], (), "out")
-    n = C if apart else 512
-    dma("s", T.y[:, 512:512 + n], T.ysb[:, 512:512 + n], ["y10", "y11", "yb1"], (), "out")
-    for k in range(4):
-        dma("ys"[k % 2], T.osc[4 * k:4 * k + 4, :], T.tcs[32 * k:32 * k + 4, :], ["t20s", "t21s"], (), "out")
+        act(T.ysb[:, 512 + a:512 + a + n], bank(b, n), F.Copy, 1.0, 0.0, (), ["y1%d" % h], (b,))
+        copy(a, n, b + 1, "y0%d" % h)
+    a, n = (H, C) if early else (0, 512)
+    if early:
+        dma("y", T.y[:, 512:512 + a], T.ysb[:, 512:512 + a], ["y10"], (), "out")
+        dma("y", T.y[:, 0:a], T.ysb[:, 0:a], ["y00"], (), "out")
+    dma("y", T.y[:, a:n], T.ysb[:, a:n], ["y00", "y01", "yb0"], (), "out")
+    dma("s", T.y[:, 512 + a:512 + n], T.ysb[:, 512 + a:512 + n], ["y10", "y11", "yb1"], (), "out")
 
-    emit(pl, queues, T, [("g", "sent"), ("y", "out")])
+    emit(pl, queues, T, [("g", "sent"), ("g", "outg"), ("y", "out")])

from concourse.bass import DstId, RemoteDMATransfer
from concourse.mybir import dt, AluOpType as A, ActivationFunctionType as F

C = 384
N = 4
LAST = N - 1
BIG = 1.5 * 2.0 ** 28
OPT = {"w1": 1, "once": -1, "pieces": 1, "load": 0, "H": 160, "cut": 96}

SCRATCH = {"ps": ("psum", [128, 4096], "float32")}
for _n, _w in (("xt", 1536), ("bt", 512), ("wt", 1024), ("rr", 128), ("fm", 128), ("dd", 128),
               ("one", 516), ("uu", 516), ("jt", 1536), ("th", 516), ("tv", 516), ("qt", 516),
               ("xd", 256), ("xa", 128), ("ww", 2560), ("at", 512), ("vt", 512), ("dz", 384), ("sg", 128)):
    SCRATCH[_n] = ("sbuf", [128, _w], "bfloat16")
for _n, _w in (("pc", 512), ("pr", 384), ("la", 384), ("sel", 128), ("cs", 128), ("tl", 768), ("val", 128), ("vr", 128),
               ("selt", 384), ("cl", 32), ("pas", 256), ("ysb", 1024)):
    SCRATCH[_n] = ("sbuf", [128, _w], "float32")
for _n, _w in (("wa", 512), ("wb", 512), ("tc", 384), ("b0", 128), ("b1q", 128), ("b1l", 128), ("b2q", 128),
               ("b2l", 128), ("p1", 128), ("p2", 128), ("l1", 512), ("l2", 512), ("l3", 512), ("jq", 512), ("eq", 512),
               ("zq", 256), ("t2q", 128), ("t3q", 128), ("w2q", 128), ("w3q", 128), ("w4q", 128), ("wq", 256),
               ("j1", 384), ("rq", 384)):
    SCRATCH[_n] = ("sbuf", [128, _w], "float8_e4m3fn_x4")
    SCRATCH[_n + "s"] = ("sbuf", [128, _w], "uint8")
for _n, _w in (("off1", 8), ("off2", 8), ("tof1", 24), ("tof2", 24)):
    SCRATCH[_n] = ("sbuf", [128, _w], "uint16")

SEMAPHORES = ["cv", "cs", "cp", "cg", "db", "dx0", "dx1", "dx2", "dw", "out", "outg", "sent",
              "ar0", "ar1", "ar2", "ar3", "arb"]
COUNTER = {"v": "cv", "s": "cs", "p": "cp", "g": "cg"}


def make_plan():
    return {"ops": [], "wr": {}, "rd": {}, "bank": {}, "n": {}}


def note(pl, q, fn, reads=(), writes=(), banks=(), sem=None, inc=0):
    deps = []
    for k in reads:
        if k in pl["wr"]:
            deps.append(pl["wr"][k])
    for k in writes:
        if k in pl["wr"]:
            deps.append(pl["wr"][k])
        deps.extend(pl["rd"].get(k, []))
    for b in banks:
        if b in pl["bank"] and pl["bank"][b][1] != q:
            deps.append(pl["bank"][b])
    if sem is None:
        pl["n"][q] = pl["n"].get(q, 0) + 1
        tok = ("c", q, pl["n"][q])
    else:
        pl["n"][sem] = pl["n"].get(sem, 0) + inc
        tok = ("d", sem, pl["n"][sem])
    pl["ops"].append((q, fn, deps, tok))
    for k in reads:
        pl["rd"].setdefault(k, []).append(tok)
    for k in writes:
        pl["wr"][k] = tok
        pl["rd"][k] = []
    for b in banks:
        pl["bank"][b] = tok
    return tok


def emit(pl, queues, T, ends):
    known, clock, waits, needed = {}, {}, [], set()
    for q, fn, deps, tok in pl["ops"]:
        kn = known.setdefault(q, {})
        best = {}
        for d in deps:
            best[d[:2]] = max(best.get(d[:2], 0), d[2])
        order = sorted(best.items(), key=lambda e: -len(clock.get(e[0] + (e[1],), {})))
        mine = []
        for key, val in order:
            if kn.get(key, 0) >= val:
                continue
            mine.append(key + (val,))
            kn[key] = val
            for k2, v2 in clock.get(key + (val,), {}).items():
                kn[k2] = max(kn.get(k2, 0), v2)
        waits.append(mine)
        needed.update(w for w in mine if w[0] == "c")
        clock[tok] = dict(kn)
    count, seen = {}, {}
    for q, fn, deps, tok in pl["ops"]:
        if tok in needed:
            seen[q] = seen.get(q, 0) + 1
            count[tok] = seen[q]
    for (q, fn, deps, tok), mine in zip(pl["ops"], waits):
        for w in mine:
            if w[0] == "c":
                queues[q].wait_ge(T.sem[COUNTER[w[1]]], count[w])
            else:
                queues[q].wait_ge(T.sem[w[1]], w[2])
        ins = fn()
        if tok in needed:
            ins.then_inc(T.sem[COUNTER[q]], 1)
    for q, sem in ends:
        if pl["n"].get(sem, 0):
            queues[q].wait_ge(T.sem[sem], pl["n"][sem])


def rank_program(g, core, T, topo):
    rank = T.rank_of(core)
    if rank is None:
        return
    cores = list(T.cores)
    V, S, P, Y = g.vector, g.scalar, g.tensor, g.sync
    queues = {"v": V, "s": S, "p": P, "g": g, "y": Y}
    pl = make_plan()
    u8, u32 = dt.uint8, dt.uint32

    def bank(b, n=128):
        return T.ps[:, 512 * b:512 * b + n]

    def col(i):
        return T.cl[:, i:i + 1]
    JB, HH, T1, P2, Q32, NPM, CORR, LIM = range(8)

    def slot(buf, piece, t, pieces=1):
        return T[buf][:, 512 * piece + t:512 * (piece + pieces):4]

    T2, W2, W3, W4, T3 = range(5)

    def tile(piece):
        return T.ww[:, 512 * piece:512 * piece + 512]

    def ts(out, in0, s1, s2, op0, op1, r, w, banks=()):
        if op1 is None:
            note(pl, "v", lambda: V.tensor_scalar(out, in0, s1, None, op0), r, w, banks)
        else:
            note(pl, "v", lambda: V.tensor_scalar(out, in0, s1, s2, op0, op1), r, w, banks)

    def act(out, in_, func, scale, bias, r, w, banks=(), accum=None):
        if accum is None:
            note(pl, "s", lambda: S.activation(out, in_, func, bias=bias, scale=scale), r, w, banks)
        else:
            note(pl, "s", lambda: S.activation(out, in_, func, bias=bias, scale=scale, accum_out=accum), r, w, banks)

    def fill(ap, c, w):
        note(pl, "v", lambda: V.memset(ap, c), (), w)

    def scan(out, d0, d1, init, op0, op1, r, w, banks=()):
        note(pl, "v", lambda: V.tensor_tensor_scan(out, d0, d1, init, op0, op1), r, w, banks)

    def quant(name, a, n, src, r, w):
        note(pl, "v", lambda: V.quantize_mx(T[name][:, a:a + n], T[name + "s"][:, a:a + n], src), r, w)

    def mm(b, st, sa, mv, ma, n, start, stop, r):
        note(pl, "p", lambda: P.matmul_mx(bank(b, n), T[st][:, sa:sa + 128], T[st + "s"][:, sa:sa + 128],
                                          T[mv][:, ma:ma + n], T[mv + "s"][:, ma:ma + n], start, stop), r, (), (b,))

    def pick(dst, a, n, win, wn, off, r, w, first=0):
        o = T[off][:, (a - first) // 16:(a - first + n) // 16]
        note(pl, "v", lambda: V.tensor_copy(T[dst][:, a:a + n].bitcast(u32),
                                            T[win][:, 0:wn].bitcast(u32).indirect(o)), r, [w + "c"])
        note(pl, "s", lambda: S.activation(T[dst + "s"][:, a:a + n], T[win + "s"][:, 0:wn].indirect(o), F.Copy),
             r, [w + "s"])

    def dma(q, out, in_, r, w, sem):
        note(pl, q, lambda: queues[q].dma_start(out, in_).then_inc(T.sem[sem], 16), r, w, sem=sem, inc=16)

    def lanes(src, dsts, part=None):
        es = [e for e in topo.engines(cores[src], cores[dsts[0]])
              if all(e in topo.engines(cores[src], cores[d]) for d in dsts)]
        if part is not None:
            es = es[part::2]
        return sum(1 << e for e in es), len(es)

    def write(src, dst, dsts, sem, r, part=None):
        m, n = lanes(rank, dsts, part)
        ids = [DstId(rid=topo.addr(cores[d])[0], pnc=topo.addr(cores[d])[1]) for d in dsts]
        tr = RemoteDMATransfer(dst_ids=ids, dma_engine_mask=m, remote_sem=T.sem[sem], src=src,
                               dsts=[dst for d in dsts])
        note(pl, "g", lambda: g.remote_dma_fused([tr], local_sem=T.sem.sent), r, (), sem="sent", inc=n)

    def send_once(name, land, dsts, sem, keys):
        ids = [DstId(rid=topo.addr(cores[d])[0], pnc=topo.addr(cores[d])[1]) for d in dsts]
        sides = [(T[name][:, C:512].bitcast(u8), T[land][:, C:512].bitcast(u8)), (T[name + "s"][:], T[land + "s"][:])]
        trs = [RemoteDMATransfer(dst_ids=ids, dma_engine_mask=lanes(rank, dsts, part)[0], remote_sem=T.sem[sem],
                                 src=src, dsts=[dst for d in dsts]) for part, (src, dst) in enumerate(sides)]
        note(pl, "g", lambda: g.remote_dma_fused(trs, local_sem=T.sem.sent), keys, (), sem="sent",
             inc=lanes(rank, dsts)[1])

    def calls(src, dsts, first):
        if first and OPT["w1"] == 1:
            return [(0, dsts, 0), (1, dsts, 1)]
        if first and OPT["w1"] == 2:
            return [(0, dsts[:2], 0), (1, dsts, 1)] + ([(0, dsts[2:], 1)] if dsts[2:] else [])
        if first and OPT["w1"] == 4:
            later = [(0, [2], 1)] if 2 in dsts else []
            return [(0, [d for d in dsts if d != 2], 0), (1, dsts, 1)] + later
        if first and OPT["w1"] == 3:
            return [(0, dsts[:1], 0), (0, dsts[1:2], 1), (1, dsts, None)] + ([(0, dsts[2:], None)] if dsts[2:] else [])
        return [(0, dsts, None), (1, dsts, None)]

    def send(name, land, a, dsts, sem, keys, first):
        for kind, ds, part in calls(rank, dsts, first):
            if kind != 1:
                c, d = {0: (0, 128), 2: (0, OPT["cut"]), 3: (OPT["cut"], 128)}[kind]
                write(T[name][:, c:d].bitcast(u8), T[land][:, a + c:a + d].bitcast(u8), ds, sem, keys[:1], part)
            else:
                write(T[name + "s"][:], T[land + "s"][:, a:a + 128], ds, sem, keys[-1:], part)

    def arrives(key, sem, src, dsts, first):
        n = sum(lanes(src, ds, part)[1] for kind, ds, part in calls(src, dsts, first) if rank in ds)
        pl["wr"][key] = ("d", sem, n)

    if OPT["load"] == 0:
        dma("y", T.bt[:], T.b[:], (), ["bt"], "db")
        dma("y", T.xt[:, 0:1024], T.x[:, 0:1024], (), ["xt0", "xt1"], "dx0")
        dma("y", T.xt[:, 1024:1536], T.x[:, 1024:1536], (), ["xt2"], "dx2")
    else:
        dma("y", T.bt[:], T.b[:], (), ["bt"], "db")
        dma("s", T.xt[:, 0:512], T.x[:, 0:512], (), ["xt0"], "dx0")
        dma("y", T.xt[:, 512:1024], T.x[:, 512:1024], (), ["xt1"], "dx1")
        dma("y", T.xt[:, 1024:1536], T.x[:, 1024:1536], (), ["xt2"], "dx2")
    dma("y", T.wt[:], T.w[:], ["xt1", "xt2"], ["wt"], "dw")

    def iota(out, pat, base, cm, w):
        note(pl, "g", lambda: g.iota(out, pat, base, cm, allow_small_or_imprecise_dtypes=True), (), w)

    def sel_g(out, in_, pat, op, c, base, cm, r, w):
        note(pl, "g", lambda: g.affine_select(out, in_, pat, op, c, base, cm), r, w)

    def const(out, n, c, w):
        act(out, T.one[:, 0:n], F.Copy, c, 0.0, ["one"], w)

    fill(T.one[:], 1.0, ["one"])
    iota(T.dd[:], [[1, 128]], 0, -1, ["dd"])
    iota(col(P2), [[1, 1]], -15, 2, ["p2c"])
    iota(T.rr[:], [[1, 128]], 0, 0, ["rr"])

    fill(slot("jt", 1, 0, 2), 0.0, ["jz0"])
    fill(slot("jt", 0, 2, 2), 0.0, ["jz1"])
    const(slot("jt", 0, 1), 128, 0.0, ["jz2"])
    const(slot("jt", 2, 1), 128, 0.0, ["jz3"])
    const(T.th[:, 3:516:4], 129, 0.25, ["th3"])
    for i in range(3):
        ts(slot("jt", i, i), T.dd[:], 0.0, 0.25, A.is_equal, A.mult, ["dd"], ["ji%d" % i])
        ts(slot("jt", i, 3), T.dd[:], 0.0, float(i), A.is_ge, A.add, ["dd"], ["jn%d" % i])
    sel_g(slot("ww", W2, 2), slot("jt", 0, 3), [[1, 128]], A.not_equal, 256.0, 0, -1, ["jn0"], ["w2s2"])
    iota(T.xd[:], [[1, 128], [0, 2]], 0, -1, ["xd"])
    iota(T.fm[:], [[0, 8], [2, 16]], -15, 0, ["fm"])
    const(T.qt[:], 516, 0.25, ["qt"])
    sel_g(T.uu[:], T.qt[:], [[1, 516]], A.is_equal, 0.0, -3, -4, ["qt"], ["uu"])
    fill(T.th[:, 0:3], 1.0, ["th"])
    const(T.dz[:, 0:1], 1, 0.0, ["dz0"])
    const(slot("ww", W2, 0), 128, 0.25, ["w2s0"])
    const(T.ww[:, 513:1024:2], 256, 0.0, ["w2z"])
    const(slot("ww", W3, 0, 2), 256, 1.0, ["ws0"])
    iota(T.vr[:], [[1, 128]], C, 0, ["vr"])
    iota(T.tl[:, 0:C], [[1, C]], 0, 0, ["tl0"])

    def later_constants():
        quant("w2q", 0, 128, tile(W2), ["w2s0", "w2z", "w2s2"], ["w2q"])
        ts(col(Q32), col(P2), BIG, -BIG, A.add, A.add, ["p2c"], ["q32"])
        fill(slot("ww", W3, 2, 3), 0.0, ["z2"])
        ts(col(NPM), col(P2), -1.0, col(Q32), A.mult, A.add, ["q32", "p2c"], ["npm"])

    def latch_constants():
        act(T.sg[:], T.fm[:], F.Sign, 1.0, col(NPM), ["fm", "npm"], ["sg"])
        act(col(CORR), col(NPM), F.Identity, 512.0, 7680.0, ["npm"], ["corr"])
        act(T.cs[:], T.sg[:], F.Identity, 33792.0, -32768.0, ["sg"], ["cs"])

    def rounded(value, t, key, name):
        act(col(t), col(value), F.Identity, 1.0, BIG, [key], [name + "t"])

    def digits(piece, value, t, key, name):
        act(slot("ww", piece, 1), T.one[:, 0:128], F.Identity, -BIG, col(t), ["one", name + "t"], [name + "1"])
        act(slot("ww", piece, 3), slot("ww", piece, 1), F.Identity, -1.0, col(value), [name + "1", key], [name + "2"])

    def copy(a, n, b, key):
        note(pl, "v", lambda: V.tensor_copy(T.ysb[:, a:a + n], bank(b, n)), (), [key], (b,))

    def quant_e(b):
        quant("eq", 128 * b, 128, T.uu[:, 3 - b:515 - b], ["uu"], ["e%d" % b])

    def quant_x(i):
        quant("wa", 128 * i, 128, T.xt[:, 512 * i:512 * i + 512], ["xt%d" % i], ["t0p%d" % i])

    def quant_w():
        quant("wq", 0, 256, T.wt[:], ["wt"], ["wq"])

    def running(i, b):
        scan(T.pc[:, 128 * i:128 * i + 128], bank(b), T.one[:, 0:128], -1e29, A.max, A.mult, ["one"], ["pc%d" % i], (b,))

    def step(buf, i):
        a = 128 * i
        act(T[buf][:, 4 + i:516:4], T.pc[:, a:a + 128], F.Sign, -1.0, T.pc[:, a + 127:a + 128], ["pc%d" % i],
            [buf + str(i)])

    pat, pkeys = "b0", ["b0"]
    tkeys = [["t0p0"], ["t0p1"], ["t0p2"]]
    for t in range(2):
        tab, pk, off, tof = ("wa", "p1", "off1", "tof1") if t == 0 else ("wb", "p2", "off2", "tof2")
        land = "l1" if t == 0 else "l2"
        tall = sorted(set(tkeys[0] + tkeys[1] + tkeys[2]))
        summers = [r for r in range(N) if r != LAST] if t == 0 else [LAST]

        def places(i):
            mm(i, tab, 128 * i, pat, 0, 128, True, True, tkeys[i] + pkeys)

        if t == 0:
            quant("b0", 0, 128, T.bt[:], ["bt"], ["b0"])
            quant("jq", 0, C, T.jt[:], ["jz0", "jz1", "jz2", "jz3", "ji0", "ji1", "ji2", "jn0", "jn1", "jn2"], ["jq"])
            quant_x(0)
            places(0)
            quant_x(1)
            places(1)
            quant_x(2)
            places(2)
            mm(3, pat, 0, tab, 0, C, True, True, tall + pkeys)
            for i in range(3):
                running(i, i)
                step("th", i)
        gb, zb = (3, 4) if t == 0 else (5, 3)
        scan(T.pr[:], bank(gb, C), T.one[:, 0:C], -1e29, A.max, A.mult, ["one"], ["pr"], (gb,))
        act(T.dz[:, 1:C], T.pr[:, 0:C - 1], F.Sign, -1.0, T.pr[:, C - 1:C], ["pr"], ["dz", "jb"], accum=col(JB))
        buf, turn, keys = ("th", "jq", ["jq"]) if t == 0 else ("tv", "j1", ["j0c", "j0s", "j1c", "j1s"])
        for n in range(2):
            quant("zq", 128 * n, 128, T[buf][:, 4 * n:4 * n + 512], [buf + str(i) for i in range(4)] + [buf], ["zq%d" % n])
            mm(zb, "zq", 128 * n, turn, 0, C, t == 0 and n == 0, n == 1, ["zq%d" % n] + keys)
        if t == 0:
            later_constants()
        rounded(JB, T1, "jb", "w3")
        act(T.xa[:], T.rr[:], F.Relu, -1.0, col(JB), ["rr", "jb"], ["xa"])
        act(col(HH), col(JB), F.Identity, -0.5, -0.75, ["jb"], ["hh"])
        if t == 0:
            const(T.ww[:, 1:512:2], 256, 0.0, ["z13"])
        act(slot("ww", W3, 1), T.one[:, 0:128], F.Identity, -BIG, col(T1), ["one", "w3t"], ["w31"])
        scan(T.la[:], T.dz[:], bank(zb, C), 1e4, A.add, A.min, ["dz", "dz0"], ["la"], (zb,))
        f = T.la[:, C - 1:C]
        ts(slot("ww", T2, 0), T.xa[:], col(HH), f, A.subtract, A.is_equal, ["xa", "hh", "la"], ["t2s0"])
        act(slot("ww", T2, 2), T.one[:, 0:128], F.Abs, f, col(HH), ["one", "hh", "la"], ["t2s2"])
        act(slot("ww", W3, 3), slot("ww", W3, 1), F.Identity, -1.0, col(JB), ["w31", "jb"], ["w32"])
        if t == 0:
            act(col(LIM), col(P2), F.Identity, 0.125, 65.875, ["p2c"], ["lim"])
            latch_constants()
            const(slot("ww", W4, 1), 128, 512.0, ["w41"])
            const(slot("ww", W4, 3), 128, 0.0, ["w42"])
            for i in range(3):
                const(slot("jt", i, i), 128, 0.0, ["ji%d" % i])
            act(slot("jt", 0, 3, 3), slot("jt", 0, 3, 3), F.Copy, 2.0, 0.0, (), ["jn0", "jn1", "jn2"])
        quant("t2q", 0, 128, tile(T2), ["t2s0", "t2s2", "z13"], ["t2q"])
        mm(5, "t2q", 0, "w2q", 0, 128, True, True, ["t2q", "w2q"])
        ts(T.ww[:, 512 * T3 + 1:512 * T3 + 512:2], T.xd[:], col(HH), f, A.subtract, A.is_equal, ["xd", "hh", "la"],
           ["t3s"])
        quant("w3q", 0, 128, tile(W3), ["ws0", "z2", "w31", "w32"], ["w3q"])
        ts(slot("ww", T3, 0), bank(5), col(LIM), None, A.is_gt, None, ["lim"], ["t3s0"], (5,))
        quant("t3q", 0, 128, tile(T3), ["t3s0", "t3s", "z2"], ["t3q"])
        mm(6, "w3q", 0, "t3q", 0, 128, True, True, ["w3q", "t3q"])
        if t == 0:
            quant("w4q", 0, 128, tile(W4), ["ws0", "z2", "w41", "w42"], ["w4q"])
            quant_e(0)
        mm(7, "w4q", 0, "t3q", 0, 128, True, True, ["w4q", "t3q"])
        scan(T.sel[:], T.cs[:], bank(6), 0.0, A.add, A.max, ["cs"], ["sel"], (6,))
        ts(T[off][:], T.sel[:, 15:128:16], col(CORR), None, A.subtract, None, ["sel", "corr"], [off])
        once = t == 1 and rank == OPT["once"]
        own = [pk + "c", pk + "s"]
        pk, pa = ("jq", C) if once else (pk, 0)
        pick(pk, pa, 128, tab, C, off, tall + [off], own[0][:-1], pa)

        dsts = [r for r in summers if r != rank]
        if once:
            send_once(pk, "l3", dsts, "ar%d" % rank, own + ["jq"])
        elif dsts:
            send(pk, land, 128 * rank, dsts, "ar%d" % rank, own, t == 0)

        if t == 0:
            iota(T.tl[:, C:2 * C], [[1, C]], 0, 0, ["tl1"])

        def values():
            note(pl, "v", lambda: V.tensor_tensor(T.val[:], bank(7), T.vr[:], A.min), ["vr"], ["val"], (7,))

        def list_out(t=t):
            act(T.pas[0:1, 128 * t:128 * t + 128], T.ps[0:1, 3072:3200], F.Copy, 1.0, 0.0, (), ["pas%d" % t], (6,))

        def table_list(t=t, off=off, tof=tof):
            win = T.tl[:, C * t:C * t + C]
            note(pl, "v", lambda: V.tensor_copy(win.indirect(T[off][:]), T.val[:]), ["val", off], ["tl%d" % t])

        def table_offsets(t=t, tof=tof):
            for i in range(3):
                scan(T.selt[:, 128 * i:128 * i + 128], T.cs[:], T.tl[:, C * t + 128 * i:C * t + 128 * i + 128], 0.0,
                     A.add, A.max, ["cs", "tl%d" % t], ["selt%d" % i])
            ts(T[tof][:], T.selt[:, 15:C:16], col(CORR), None, A.subtract, None,
               ["selt0", "selt1", "selt2", "corr"], [tof])

        late = t == 1 and rank == LAST
        vb = 0 if late else 4

        def held(pk=pk, pa=pa, own=own, vb=vb):
            for b in range(4):
                mm(vb + b, "eq", 128 * b, pk, pa, 128, True, False, ["e%d" % b] + own)

        def evacuate(first, tile, c, name):
            for b in range(4):
                if b % 2 == 1:
                    ts(slot(tile, 0, b), bank(first + b), c, None, A.mult, None, (), [name + str(b)], (first + b,))
                else:
                    act(slot(tile, 0, b), bank(first + b), F.Copy, c, 0.0, (), [name + str(b)], (first + b,))
            return [name + str(b) for b in range(4)]

        if not late:
            list_out()
            values()
            if t == 0:
                quant_e(1)
                quant_e(2)
            table_list()
            if t == 0:
                quant_e(3)
            table_offsets()
            held()
            if t == 0:
                quant("rq", 0, C, T.jt[:], ["ji0", "ji1", "ji2", "jn0"], ["rq"])
                const(T.tv[:, 0:4], 4, 1.0, ["tv"])
                pick("j1", 0, C // 2, "eq", 512, tof, ["e0", "e1", "e2", "e3", tof], "j0")
            if (t == 0) == (rank == LAST):
                quant_w()

        if rank in summers:
            order = [1, 0, 2, 3] if rank == 1 else [0, 1, 2, 3]
            for n, r in enumerate(order):
                if r == rank:
                    mv, a, keys = pk, 0, own
                else:
                    arrives("land%d" % r, "ar%d" % r, r, [d for d in summers if d != r], t == 0)
                    mv, a, keys = land, 128 * r, ["land%d" % r]
                    if t == 1 and r == OPT["once"]:
                        mv, a = "l3", C
                        pl["wr"][keys[0]] = ("d", "ar%d" % r, lanes(r, [rank])[1])
                for b in range(4):
                    mm(b, "eq", 128 * b, mv, a, 128, n == 0, n == N - 1, ["e%d" % b] + keys)
            pat = "b1q" if t == 0 else "b2q"
            quant(pat, 0, 128, T.at[:], evacuate(0, "at", 1.0, "at"), [pat])
            pkeys = [pat]
        others = [r for r in range(N) if r not in summers]
        far = "b1l" if t == 0 else "b2l"
        giver = min(summers, key=lambda r: (topo.die(cores[r]) != topo.die(cores[others[0]]), -r))
        if rank == giver:
            send(pat, far, 0, others, "arb", pkeys, False)
        if rank in others:
            pat, pkeys = far, [far]
            arrives(far, "arb", giver, others, False)
        if t == 0:
            pick("j1", C // 2, C // 2, "eq", 512, tof, ["e0", "e1", "e2", "e3", tof], "j1")
        if late:
            list_out()
            values()
            held()
            table_list()
        if t == 1 and not late:
            dma("y", T.pa[:], T.pas[0:1, :], ["pas0", "pas1"], (), "out")

        if t == 0:
            mm(3, "zq", 0, "rq", 0, C, True, False, ["rq", "zq0"])
        for b in range(4):
            mm(vb + b, "eq", 128 * b, pat, 0, 128, False, True, ["e%d" % b] + pkeys)
        if t == 1:
            for o in range(2):
                mm(4 - vb + o, "wq", 128 * (1 - o), pat, 0, 128, True, True, ["wq"] + pkeys)
        if t == 0:
            for i in range(3):
                mm(i, tab, 128 * i, pat, 0, 128, True, True, tkeys[i] + pkeys)
        keys = evacuate(vb, "vt", 2.0, "vt")
        if t == 0:
            running(0, 0)
        if t == 1:
            act(T.ysb[:, 512 + C:1024], bank(4 - vb), F.Copy, 1.0, 0.0, (), ["yb1"], (4 - vb,))
        if late:
            table_offsets()
        quant(tab, C, 128, T.vt[:], keys, ["v%d" % t])
        if t == 1:
            copy(C, 128, 5 - vb, "yb0")
        if t == 0:
            mm(4, tab, C, pat, 0, 128, True, True, ["v0"] + pkeys)
            running(1, 1)
            pick("wb", 0, C, "wa", 512, tof, tall + ["v0", tof], "t1")
            tkeys = [["t1c", "t1s"]] * 3
            mm(5, pat, 0, "wb", 0, C, True, True, tkeys[0] + pkeys)
            step("tv", 0)
            step("tv", 1)
            running(3, 4)
            step("tv", 3)
            running(2, 2)
            step("tv", 2)

    def scales_out(q, ks):
        for k in ks:
            dma(q, T.osc[4 * k:4 * k + 4, :], T.tcs[32 * k:32 * k + 4, :], ["t20s", "t21s"], (), "outg" if q == "g" else "out")

    early = rank != LAST
    if early:
        for o in (1, 0):
            dma("y", T.y[:, 512 * o + C:512 * o + 512], T.ysb[:, 512 * o + C:512 * o + 512], ["yb%d" % o], (), "out")
    H = OPT["H"]
    parts = ((0, H), (H, C - H))
    for h, (a, n) in enumerate(parts):
        pick("tc", a, n, "wb", 512, "tof2", tall + ["v1", "tof2"], "t2%d" % h)
        for o in range(2):
            mm(vb + 2 * h + o, "wq", 128 * (1 - o), "tc", a, n, True, True, ["wq", "t2%dc" % h, "t2%ds" % h])
    dma("y", T.oc[:], T.tc[:].bitcast(u8), ["t20c", "t21c"], (), "out")
    if not early:
        dma("y", T.pa[:], T.pas[0:1, :], ["pas0", "pas1"], (), "out")
    scales_out("y", range(4))
    for h, (a, n) in enumerate(parts):
        b = vb + 2 * h
        act(T.ysb[:, 512 + a:512 + a + n], bank(b, n), F.Copy, 1.0, 0.0, (), ["y1%d" % h], (b,))
        copy(a, n, b + 1, "y0%d" % h)
    a, n = (H, C) if early else (0, 512)
    if early:
        dma("y", T.y[:, 512:512 + a], T.ysb[:, 512:512 + a], ["y10"], (), "out")
        dma("y", T.y[:, 0:a], T.ysb[:, 0:a], ["y00"], (), "out")
    dma("y", T.y[:, a:n], T.ysb[:, a:n], ["y00", "y01", "yb0"], (), "out")
    dma("s", T.y[:, 512 + a:512 + n], T.ysb[:, 512 + a:512 + n], ["y10", "y11", "yb1"], (), "out")

    emit(pl, queues, T, [("g", "sent"), ("g", "outg"), ("y", "out")])
